import numpy as np
import ml_dtypes


def mxq(x, axis, fmt="e4m3"):
    dtype, down = {"e4m3": (ml_dtypes.float8_e4m3fn, 7), "e5m2": (ml_dtypes.float8_e5m2, 14)}[fmt]
    v = np.moveaxis(np.asarray(x, np.float32).astype(ml_dtypes.bfloat16).astype(np.float64), axis, -1)
    blocks = v.reshape(v.shape[:-1] + (-1, 32))
    amax = np.abs(blocks).max(-1, keepdims=True)
    byte = np.maximum(np.where(amax > 0, np.frexp(amax)[1] - 1 + 127, 0) - down, 1)
    scale = np.exp2(byte - 127.0)
    codes = (blocks / scale).astype(np.float32).astype(dtype).astype(np.float64)
    return np.moveaxis((codes * scale).reshape(v.shape), -1, axis)


WIDE = False


def mx_kscale(k):
    if not WIDE:
        return np.ones(k)
    levels = np.array([10, -10, 5, -5, 0])
    if k % 512:
        return np.exp2(np.random.permutation(np.resize(levels, k // 32))).repeat(32)
    a = np.empty((k // 512, 16))
    for p in range(k // 512):
        a[p, :8] = np.random.permutation(np.resize(levels, 8))
        for g in range(8):
            far = levels[np.abs(levels - a[p, g]) >= 10]
            a[p, g + 8] = far[np.random.randint(len(far))]
    return np.exp2(a.ravel()).repeat(32)


def f64(x):
    return np.asarray(x).astype(np.float64)


def striped(idx):
    return np.tile(idx.reshape(-1, 16).T, (8, 1)).astype(np.uint16)


def unstriped(offs):
    return offs[:16].T.reshape(-1).astype(np.int64)


K, T, S, V, H, N = 1024, 1024, 768, 256, 512, 128


def setup_inputs():
    n = np.random.standard_normal
    s = mx_kscale(K)[:, None]
    u = mx_kscale(H)
    return {
        "xT": (n((K, T)) * s).astype(np.float32),
        "w1": (n((K, H)) / np.sqrt(K) / s * u).astype(np.float32),
        "w2": (n((K, H)) / np.sqrt(K) / s).astype(np.float32),
        "w3": (n((K, H)) / np.sqrt(K) / s).astype(np.float32),
        "w4": (n((H, N)) / np.sqrt(H) / u[:, None]).astype(np.float32),
        "offs": striped(np.random.permutation(T)[:S]),
    }


def reference(xT, w1, w2, w3, w4, offs):
    xq = mxq(f64(xT)[:, unstriped(offs)], 0, "e4m3")
    z = (((mxq(f64(w1), 0, "e4m3").T @ xq[:, :V])) * ((mxq(f64(w2), 0, "e4m3").T @ xq[:, V:2 * V]))) * ((mxq(f64(w3), 0, "e4m3").T @ xq[:, 2 * V:3 * V]))
    return mxq(f64(w4), 0, "e4m3").T @ mxq(z, 0, "e4m3")

@@ -1,0 +1,212 @@
+from contextlib import ExitStack
+
+import concourse.mybir as mybir
+
+K, T, S, V, H, N = 1024, 1024, 768, 256, 512, 128
+FLOPS = 2 * (3 * K * H * V + H * N * V)
+
+F32 = mybir.dt.float32
+BF16 = mybir.dt.bfloat16
+U32 = mybir.dt.uint32
+U16 = mybir.dt.uint16
+U8 = mybir.dt.uint8
+FP8X4 = mybir.dt.float8_e4m3fn_x4
+MULT = mybir.AluOpType.mult
+
+P = 128
+PACK = 4
+K_PASS = P * PACK
+PASSES = K // K_PASS
+RUN = 4
+HALF = 128
+X_VECTOR_COLS = (320, 320, 128, 256)
+
+
+def tile_picked_trilin_none_e_kernel(tc, xT, w1, w2, w3, w4, offs, out):
+    nc = tc.nc
+    weights = (w1, w2, w3)
+
+    def cast(engine, dst, src):
+        if engine == "vector":
+            nc.vector.tensor_copy(out=dst, in_=src)
+        else:
+            nc.scalar.copy(out=dst, in_=src)
+
+    with ExitStack() as ctx:
+        keep = ctx.enter_context(tc.tile_pool(name="keep", bufs=1))
+        psum = ctx.enter_context(tc.psum_pool(name="psum", bufs=1))
+
+        offsets = keep.tile([P, S // 16], U16, name="offsets")
+        x_raw = {(g, h): keep.tile([P, PACK, T // 2], F32, name="x_raw%d_%d" % (g, h)) for g in range(PASSES) for h in range(2)}
+        w_raw = {(d, g): keep.tile([P, PACK, H], F32, name="w_raw%d_%d" % (d, g), tag="w_raw%d_%d" % (d, g)) for d in range(3) for g in range(PASSES)}
+        w4_raw = keep.tile([P, PACK, N], F32, name="w4_raw")
+
+        def pass_rows(matrix, g):
+            return matrix[g * K_PASS : (g + 1) * K_PASS, :].rearrange("(p j) c -> p j c", j=PACK)
+
+        for g in range(PASSES):
+            for h in range(2):
+                nc.sync.dma_start(out=x_raw[g, h][:], in_=pass_rows(xT, g)[:, :, h * (T // 2) : (h + 1) * (T // 2)])
+            if g == 0:
+                nc.sync.dma_start(offsets[:], offs)
+        for d in range(3):
+            for g in range(PASSES):
+                nc.sync.dma_start(out=w_raw[d, g][:], in_=pass_rows(weights[d], g))
+        w4_dealt = w4.rearrange("(u t q) n -> q u t n", t=PACK, q=RUN)
+        for q in range(RUN):
+            nc.sync.dma_start(out=w4_raw[q:P:RUN, :, :], in_=w4_dealt[q])
+
+        warm = keep.tile([P, 8], F32, name="warm")
+        warm_out = keep.tile([P, 8], BF16, name="warm_out")
+        nc.vector.memset(warm[:], 0.0)
+        nc.scalar.copy(out=warm_out[:], in_=warm[:])
+        x_scales = keep.tile([P, T], U8, name="x_scales", align_bytes=64)
+        nc.gpsimd.memset(x_scales[:], 0)
+        picked_words = []
+        for g in range(PASSES):
+            x_words = keep.tile([P, T], U32, name="x_words%d" % g, align_bytes=64)
+            halves = [keep.tile([P, T // 2, PACK], BF16, name="x_bf%d_%d" % (g, h), align_bytes=64) for h in range(2)]
+
+            for h in range(2):
+                dst = halves[h][:].rearrange("p (c r) j -> p c j r", r=RUN)
+                src = x_raw[g, h][:].rearrange("p j (c r) -> p c j r", r=RUN)
+                split = X_VECTOR_COLS[2 * g + h] // RUN
+                cast("vector", dst[:, :split], src[:, :split])
+                cast("scalar", dst[:, split:], src[:, split:])
+                cols = slice(h * (T // 2), (h + 1) * (T // 2))
+                nc.vector.quantize_mx(
+                    out=x_words[:, cols].bitcast(FP8X4),
+                    scales=x_scales[4 * g : P, cols],
+                    in_=halves[h][:].rearrange("p c j -> p (c j)"),
+                )
+            words = keep.tile([P, S], U32, name="picked_words%d" % g, align_bytes=64)
+            nc.vector.tensor_copy(words[:], x_words[:].indirect(offsets[:]))
+            picked_words.append(words)
+        picked_scales = keep.tile([P, S], U8, name="picked_scales", align_bytes=64)
+        nc.vector.tensor_copy(picked_scales[:], x_scales[:].indirect(offsets[:]))
+
+        w_words = {}
+        w_scales = {}
+
+        def cast_w(d, g, t0, t1, parts):
+            nt = t1 - t0
+            grouped = keep.tile([P, nt, P, PACK], BF16, name="w_bf%d_%d_%d" % (d, g, t0), tag="w_bf%d_%d_%d" % (d, g, t0), align_bytes=64)
+            dst = grouped[:].rearrange("p t (u q) j -> p t u j q", q=RUN)
+            src = w_raw[d, g][:].rearrange("p j (u t q) -> p t u j q", t=PACK, q=RUN)
+            for engine, u0, u1 in parts:
+                cast(engine, dst[:, :, u0:u1, :, :], src[:, t0:t1, u0:u1, :, :])
+            return grouped
+
+        def quantise_w(d, g, t0, t1, grouped):
+            nt = t1 - t0
+            words = keep.tile([P, nt * P], U32, name="w_words%d_%d_%d" % (d, g, t0), align_bytes=64)
+            scales = keep.tile([P, nt * P], U8, name="w_scales%d_%d_%d" % (d, g, t0), align_bytes=64)
+            nc.vector.quantize_mx(
+                out=words[:].bitcast(FP8X4), scales=scales[:], in_=grouped[:].rearrange("p t m j -> p (t m j)")
+            )
+            for t in range(t0, t1):
+                cols = slice((t - t0) * P, (t - t0 + 1) * P)
+                w_words[d, g, t] = words[:, cols]
+                w_scales[d, g, t] = scales[:, cols]
+
+        banks = {(d, h): psum.tile([P, PACK, HALF], F32, name="bank%d_%d" % (d, h)) for d in range(3) for h in range(2)}
+
+        def product(d):
+            for h in range(2):
+                cols = slice(d * V + h * HALF, d * V + (h + 1) * HALF)
+                for t in range(PACK):
+                    for g in range(PASSES):
+                        nc.tensor.matmul_mx(
+                            out=banks[d, h][:, t, :],
+                            lhsT=w_words[d, g, t].bitcast(FP8X4),
+                            lhsT_scale=w_scales[d, g, t],
+                            rhs=picked_words[g][:, cols].bitcast(FP8X4),
+                            rhs_scale=picked_scales[4 * g : P, cols],
+                            start=(g == 0),
+                            stop=(g == PASSES - 1),
+                        )
+
+        def turned(d, h):
+            return banks[d, h][:].rearrange("p t v -> p v t")
+
+        U = P // RUN
+        whole_s = [("scalar", 0, U)]
+        whole_v = [("vector", 0, U)]
+
+        def cast_shared(d, g, n_vector):
+            grouped = keep.tile([P, PACK, P, PACK], BF16, name="w_bf%d_%d" % (d, g), align_bytes=64)
+            dst = grouped[:].rearrange("p t (u q) j -> p t u j q", q=RUN)
+            src = w_raw[d, g][:].rearrange("p j (u t q) -> p t u j q", t=PACK, q=RUN)
+            if n_vector:
+                cast("vector", dst[:, :n_vector], src[:, :n_vector])
+            cast("scalar", dst[:, n_vector:], src[:, n_vector:])
+            return grouped
+
+        for g in range(PASSES):
+            quantise_w(0, g, 0, 4, cast_shared(0, g, 0))
+        product(0)
+        quantise_w(1, 0, 0, 4, cast_shared(1, 0, 1))
+        a = cast_w(1, 1, 0, 2, whole_v)
+        b = cast_w(1, 1, 2, 4, whole_s)
+        quantise_w(1, 1, 0, 2, a)
+        quantise_w(1, 1, 2, 4, b)
+        first_both = keep.tile([P, 2, HALF, PACK], F32, name="first", tag="w_raw1_1")
+        first = [first_both[:, h] for h in range(2)]
+        for h in range(2):
+            nc.scalar.copy(out=first[h], in_=turned(0, h))
+        product(1)
+        a = cast_w(2, 0, 0, 2, whole_v)
+        b = cast_w(2, 0, 2, 4, whole_s)
+        quantise_w(2, 0, 0, 2, a)
+        pair = [
+            keep.tile([P, HALF, PACK], F32, name="pair0", tag="w_bf2_0_0", align_bytes=64),
+            None,
+        ]
+        nc.vector.tensor_tensor(pair[0][:], turned(1, 0), first[0], MULT)
+        quantise_w(2, 0, 2, 4, b)
+
+        g0 = cast_w(2, 1, 0, 1, whole_v)
+        g1 = cast_w(2, 1, 1, 2, whole_v)
+        g2 = cast_w(2, 1, 2, 3, whole_s)
+        g3 = cast_w(2, 1, 3, 4, whole_s)
+        quantise_w(2, 1, 0, 1, g0)
+        quantise_w(2, 1, 1, 2, g1)
+        quantise_w(2, 1, 2, 3, g2)
+        quantise_w(2, 1, 3, 4, g3)
+        pair[1] = keep.tile([P, HALF, PACK], F32, name="pair1", tag="w_bf2_1_2", align_bytes=64)
+        nc.vector.tensor_tensor(pair[1][:], turned(1, 1), first[1], MULT)
+        product(2)
+
+        w4_bf = keep.tile([P, N, PACK], BF16, name="w4_bf", align_bytes=64)
+        nc.scalar.copy(
+            out=w4_bf[:].rearrange("p (c r) t -> p c t r", r=RUN),
+            in_=w4_raw[:].rearrange("p t (c r) -> p c t r", r=RUN),
+        )
+        w4_words = keep.tile([P, N], U32, name="w4_words", align_bytes=64)
+        w4_scales = keep.tile([P, N], U8, name="w4_scales", align_bytes=64)
+        nc.vector.quantize_mx(
+            out=w4_words[:].bitcast(FP8X4), scales=w4_scales[:], in_=w4_bf[:].rearrange("p n t -> p (n t)")
+        )
+
+        z = [keep.tile([P, HALF, PACK], BF16, name="z%d" % h, align_bytes=64) for h in range(2)]
+        for h in range(2):
+            nc.vector.tensor_tensor(z[h][:], turned(2, h), pair[h][:], MULT)
+        for h in range(2):
+            z_words = keep.tile([P, HALF], U32, name="z_words%d" % h, align_bytes=64)
+            z_scales = keep.tile([P, HALF], U8, name="z_scales%d" % h, align_bytes=64)
+            nc.vector.quantize_mx(
+                out=z_words[:].bitcast(FP8X4), scales=z_scales[:], in_=z[h][:].rearrange("p v t -> p (v t)")
+            )
+            acc = psum.tile([P, HALF], F32, name="acc%d" % h)
+            nc.tensor.matmul_mx(
+                out=acc[:],
+                lhsT=w4_words[:].bitcast(FP8X4),
+                lhsT_scale=w4_scales[:],
+                rhs=z_words[:].bitcast(FP8X4),
+                rhs_scale=z_scales[:],
+                start=True,
+                stop=True,
+            )
+            result = keep.tile([P, HALF], F32, name="result%d" % h)
+            nc.scalar.copy(out=result[:], in_=acc[:])
+            nc.sync.dma_start(out=out[:, h * HALF : (h + 1) * HALF], in_=result[:])

@@ -19,7 +19,7 @@ K_PASS = P * PACK
 PASSES = K // K_PASS
 RUN = 4
 HALF = 128
-X_VECTOR_COLS = (320, 320, 128, 256)
+X_PIECES = ((0, 0, 512, 320), (0, 512, 1024, 320), (1, 0, 512, 128), (1, 512, 768, 0), (1, 768, 1024, 256))
 
 
 def tile_picked_trilin_none_e_kernel(tc, xT, w1, w2, w3, w4, offs, out):
@@ -37,17 +37,16 @@ def tile_picked_trilin_none_e_kernel(tc, xT, w1, w2, w3, w4, offs, out):
         psum = ctx.enter_context(tc.psum_pool(name="psum", bufs=1))
 
         offsets = keep.tile([P, S // 16], U16, name="offsets")
-        x_raw = {(g, h): keep.tile([P, PACK, T // 2], F32, name="x_raw%d_%d" % (g, h)) for g in range(PASSES) for h in range(2)}
+        x_raw = {(g, c0): keep.tile([P, PACK, c1 - c0], F32, name="x_raw%d_%d" % (g, c0)) for g, c0, c1, share in X_PIECES}
         w_raw = {(d, g): keep.tile([P, PACK, H], F32, name="w_raw%d_%d" % (d, g), tag="w_raw%d_%d" % (d, g)) for d in range(3) for g in range(PASSES)}
         w4_raw = keep.tile([P, PACK, N], F32, name="w4_raw")
 
         def pass_rows(matrix, g):
             return matrix[g * K_PASS : (g + 1) * K_PASS, :].rearrange("(p j) c -> p j c", j=PACK)
 
-        for g in range(PASSES):
-            for h in range(2):
-                nc.sync.dma_start(out=x_raw[g, h][:], in_=pass_rows(xT, g)[:, :, h * (T // 2) : (h + 1) * (T // 2)])
-            if g == 0:
+        for g, c0, c1, share in X_PIECES:
+            nc.sync.dma_start(out=x_raw[g, c0][:], in_=pass_rows(xT, g)[:, :, c0:c1])
+            if (g, c1) == (0, T):
                 nc.sync.dma_start(offsets[:], offs)
         for d in range(3):
             for g in range(PASSES):
@@ -65,19 +64,21 @@ def tile_picked_trilin_none_e_kernel(tc, xT, w1, w2, w3, w4, offs, out):
         picked_words = []
         for g in range(PASSES):
             x_words = keep.tile([P, T], U32, name="x_words%d" % g, align_bytes=64)
-            halves = [keep.tile([P, T // 2, PACK], BF16, name="x_bf%d_%d" % (g, h), align_bytes=64) for h in range(2)]
-
-            for h in range(2):
-                dst = halves[h][:].rearrange("p (c r) j -> p c j r", r=RUN)
-                src = x_raw[g, h][:].rearrange("p j (c r) -> p c j r", r=RUN)
-                split = X_VECTOR_COLS[2 * g + h] // RUN
-                cast("vector", dst[:, :split], src[:, :split])
-                cast("scalar", dst[:, split:], src[:, split:])
-                cols = slice(h * (T // 2), (h + 1) * (T // 2))
+            for piece_pass, c0, c1, share in X_PIECES:
+                if piece_pass != g:
+                    continue
+                x_bf = keep.tile([P, c1 - c0, PACK], BF16, name="x_bf%d_%d" % (g, c0), align_bytes=64)
+                dst = x_bf[:].rearrange("p (c r) j -> p c j r", r=RUN)
+                src = x_raw[g, c0][:].rearrange("p j (c r) -> p c j r", r=RUN)
+                split = share // RUN
+                if share > 0:
+                    cast("vector", dst[:, :split], src[:, :split])
+                if share < c1 - c0:
+                    cast("scalar", dst[:, split:], src[:, split:])
                 nc.vector.quantize_mx(
-                    out=x_words[:, cols].bitcast(FP8X4),
-                    scales=x_scales[4 * g : P, cols],
-                    in_=halves[h][:].rearrange("p c j -> p (c j)"),
+                    out=x_words[:, c0:c1].bitcast(FP8X4),
+                    scales=x_scales[4 * g : P, c0:c1],
+                    in_=x_bf[:].rearrange("p c j -> p (c j)"),
                 )
             words = keep.tile([P, S], U32, name="picked_words%d" % g, align_bytes=64)
             nc.vector.tensor_copy(words[:], x_words[:].indirect(offsets[:]))
@@ -142,10 +143,13 @@ def tile_picked_trilin_none_e_kernel(tc, xT, w1, w2, w3, w4, offs, out):
             cast("scalar", dst[:, n_vector:], src[:, n_vector:])
             return grouped
 
-        for g in range(PASSES):
-            quantise_w(0, g, 0, 4, cast_shared(0, g, 0))
+        quantise_w(0, 0, 0, 4, cast_shared(0, 0, 0))
+        quantise_w(0, 1, 0, 4, cast_shared(0, 1, 2))
         product(0)
-        quantise_w(1, 0, 0, 4, cast_shared(1, 0, 1))
+        a = cast_w(1, 0, 0, 2, whole_v)
+        b = cast_w(1, 0, 2, 4, whole_s)
+        quantise_w(1, 0, 2, 4, b)
+        quantise_w(1, 0, 0, 2, a)
         a = cast_w(1, 1, 0, 2, whole_v)
         b = cast_w(1, 1, 2, 4, whole_s)
         quantise_w(1, 1, 0, 2, a)
@@ -173,7 +177,7 @@ def tile_picked_trilin_none_e_kernel(tc, xT, w1, w2, w3, w4, offs, out):
         quantise_w(2, 1, 1, 2, g1)
         quantise_w(2, 1, 2, 3, g2)
         quantise_w(2, 1, 3, 4, g3)
-        pair[1] = keep.tile([P, HALF, PACK], F32, name="pair1", tag="w_bf2_1_2", align_bytes=64)
+        pair[1] = keep.tile([P, HALF, PACK], F32, name="pair1", tag="w_bf2_1_3", align_bytes=64)
         nc.vector.tensor_tensor(pair[1][:], turned(1, 1), first[1], MULT)
         product(2)
 
@@ -182,15 +186,15 @@ def tile_picked_trilin_none_e_kernel(tc, xT, w1, w2, w3, w4, offs, out):
             out=w4_bf[:].rearrange("p (c r) t -> p c t r", r=RUN),
             in_=w4_raw[:].rearrange("p t (c r) -> p c t r", r=RUN),
         )
-        w4_words = keep.tile([P, N], U32, name="w4_words", align_bytes=64)
+        z = [keep.tile([P, HALF, PACK], BF16, name="z%d" % h, align_bytes=64) for h in range(2)]
+        for h in range(2):
+            nc.vector.tensor_tensor(z[h][:], turned(2, h), pair[h][:], MULT)
+        w4_words = keep.tile([P, N], U32, name="w4_words", tag="w_bf2_0_0", align_bytes=64)
         w4_scales = keep.tile([P, N], U8, name="w4_scales", align_bytes=64)
         nc.vector.quantize_mx(
             out=w4_words[:].bitcast(FP8X4), scales=w4_scales[:], in_=w4_bf[:].rearrange("p n t -> p (n t)")
         )
 
-        z = [keep.tile([P, HALF, PACK], BF16, name="z%d" % h, align_bytes=64) for h in range(2)]
-        for h in range(2):
-            nc.vector.tensor_tensor(z[h][:], turned(2, h), pair[h][:], MULT)
         for h in range(2):
             z_words = keep.tile([P, HALF], U32, name="z_words%d" % h, align_bytes=64)
             z_scales = keep.tile([P, HALF], U8, name="z_scales%d" % h, align_bytes=64)

@@ -19,7 +19,7 @@ K_PASS = P * PACK
 PASSES = K // K_PASS
 RUN = 4
 HALF = 128
-X_PIECES = ((0, 0, 512, 320), (0, 512, 1024, 320), (1, 0, 512, 128), (1, 512, 768, 0), (1, 768, 1024, 256))
+X_PIECES = ((0, 0, 512, 512), (0, 512, 1024, 128), (1, 0, 512, 512), (1, 512, 1024, 128))
 
 
 def tile_picked_trilin_none_e_kernel(tc, xT, w1, w2, w3, w4, offs, out):
@@ -37,17 +37,16 @@ def tile_picked_trilin_none_e_kernel(tc, xT, w1, w2, w3, w4, offs, out):
         psum = ctx.enter_context(tc.psum_pool(name="psum", bufs=1))
 
         offsets = keep.tile([P, S // 16], U16, name="offsets")
-        x_raw = {(g, c0): keep.tile([P, PACK, c1 - c0], F32, name="x_raw%d_%d" % (g, c0)) for g, c0, c1, share in X_PIECES}
+        x_raw = [keep.tile([P, PACK, T], F32, name="x_raw%d" % g) for g in range(PASSES)]
         w_raw = {(d, g): keep.tile([P, PACK, H], F32, name="w_raw%d_%d" % (d, g), tag="w_raw%d_%d" % (d, g)) for d in range(3) for g in range(PASSES)}
         w4_raw = keep.tile([P, PACK, N], F32, name="w4_raw")
 
         def pass_rows(matrix, g):
             return matrix[g * K_PASS : (g + 1) * K_PASS, :].rearrange("(p j) c -> p j c", j=PACK)
 
-        for g, c0, c1, share in X_PIECES:
-            nc.sync.dma_start(out=x_raw[g, c0][:], in_=pass_rows(xT, g)[:, :, c0:c1])
-            if (g, c1) == (0, T):
-                nc.sync.dma_start(offsets[:], offs)
+        nc.sync.dma_start(out=x_raw[0][:], in_=pass_rows(xT, 0))
+        nc.sync.dma_start(offsets[:], offs)
+        nc.sync.dma_start(out=x_raw[1][:], in_=pass_rows(xT, 1))
         for d in range(3):
             for g in range(PASSES):
                 nc.sync.dma_start(out=w_raw[d, g][:], in_=pass_rows(weights[d], g))
@@ -69,7 +68,7 @@ def tile_picked_trilin_none_e_kernel(tc, xT, w1, w2, w3, w4, offs, out):
                     continue
                 x_bf = keep.tile([P, c1 - c0, PACK], BF16, name="x_bf%d_%d" % (g, c0), align_bytes=64)
                 dst = x_bf[:].rearrange("p (c r) j -> p c j r", r=RUN)
-                src = x_raw[g, c0][:].rearrange("p j (c r) -> p c j r", r=RUN)
+                src = x_raw[g][:, :, c0:c1].rearrange("p j (c r) -> p c j r", r=RUN)
                 split = share // RUN
                 if share > 0:
                     cast("vector", dst[:, :split], src[:, :split])
@@ -144,7 +143,7 @@ def tile_picked_trilin_none_e_kernel(tc, xT, w1, w2, w3, w4, offs, out):
             return grouped
 
         quantise_w(0, 0, 0, 4, cast_shared(0, 0, 0))
-        quantise_w(0, 1, 0, 4, cast_shared(0, 1, 2))
+        quantise_w(0, 1, 0, 4, cast_shared(0, 1, 0))
         product(0)
         a = cast_w(1, 0, 0, 2, whole_v)
         b = cast_w(1, 0, 2, 4, whole_s)

@@ -161,6 +161,17 @@ def tile_picked_trilin_none_e_kernel(tc, xT, w1, w2, w3, w4, offs, out):
         a = cast_w(2, 0, 0, 2, whole_v)
         b = cast_w(2, 0, 2, 4, whole_s)
         quantise_w(2, 0, 0, 2, a)
+        idle = psum.tile([P, 512], F32, name="idle", tag="acc0")
+        for rep in range(3):
+            nc.tensor.matmul_mx(
+                out=idle[:],
+                lhsT=w_words[2, 0, 1].bitcast(FP8X4),
+                lhsT_scale=w_scales[2, 0, 1],
+                rhs=picked_words[0][:, 0:512].bitcast(FP8X4),
+                rhs_scale=picked_scales[:, 0:512],
+                start=True,
+                stop=True,
+            )
         pair = [
             keep.tile([P, HALF, PACK], F32, name="pair0", tag="w_bf2_0_0", align_bytes=64),
             None,
@@ -200,7 +211,7 @@ def tile_picked_trilin_none_e_kernel(tc, xT, w1, w2, w3, w4, offs, out):
             nc.vector.quantize_mx(
                 out=z_words[:].bitcast(FP8X4), scales=z_scales[:], in_=z[h][:].rearrange("p v t -> p (v t)")
             )
-            acc = psum.tile([P, HALF], F32, name="acc%d" % h)
+            acc = psum.tile([P, HALF], F32, name="acc%d" % h, tag="acc%d" % h)
             nc.tensor.matmul_mx(
                 out=acc[:],
                 lhsT=w4_words[:].bitcast(FP8X4),

@@ -54,10 +54,6 @@ def tile_picked_trilin_none_e_kernel(tc, xT, w1, w2, w3, w4, offs, out):
         for q in range(RUN):
             nc.sync.dma_start(out=w4_raw[q:P:RUN, :, :], in_=w4_dealt[q])
 
-        warm = keep.tile([P, 8], F32, name="warm")
-        warm_out = keep.tile([P, 8], BF16, name="warm_out")
-        nc.vector.memset(warm[:], 0.0)
-        nc.scalar.copy(out=warm_out[:], in_=warm[:])
         x_scales = keep.tile([P, T], U8, name="x_scales", align_bytes=64)
         nc.gpsimd.memset(x_scales[:], 0)
         picked_words = []
@@ -111,19 +107,19 @@ def tile_picked_trilin_none_e_kernel(tc, xT, w1, w2, w3, w4, offs, out):
 
         banks = {(d, h): psum.tile([P, PACK, HALF], F32, name="bank%d_%d" % (d, h)) for d in range(3) for h in range(2)}
 
-        def product(d):
-            for h in range(2):
-                cols = slice(d * V + h * HALF, d * V + (h + 1) * HALF)
-                for t in range(PACK):
-                    for g in range(PASSES):
+        def product(d, g):
+            for t in range(PACK):
+                for h in range(2):
+                    cols = slice(d * V + h * HALF, d * V + (h + 1) * HALF)
+                    if True:
                         nc.tensor.matmul_mx(
                             out=banks[d, h][:, t, :],
                             lhsT=w_words[d, g, t].bitcast(FP8X4),
                             lhsT_scale=w_scales[d, g, t],
                             rhs=picked_words[g][:, cols].bitcast(FP8X4),
                             rhs_scale=picked_scales[4 * g : P, cols],
-                            start=(g == 0),
-                            stop=(g == PASSES - 1),
+                            start=(g == 0 and t == 0),
+                            stop=(g == PASSES - 1 and t == PACK - 1),
                         )
 
         def turned(d, h):
@@ -143,12 +139,14 @@ def tile_picked_trilin_none_e_kernel(tc, xT, w1, w2, w3, w4, offs, out):
             return grouped
 
         quantise_w(0, 0, 0, 4, cast_shared(0, 0, 0))
+        product(0, 0)
         quantise_w(0, 1, 0, 4, cast_shared(0, 1, 0))
-        product(0)
+        product(0, 1)
         a = cast_w(1, 0, 0, 2, whole_v)
         b = cast_w(1, 0, 2, 4, whole_s)
         quantise_w(1, 0, 2, 4, b)
         quantise_w(1, 0, 0, 2, a)
+        product(1, 0)
         a = cast_w(1, 1, 0, 2, whole_v)
         b = cast_w(1, 1, 2, 4, whole_s)
         quantise_w(1, 1, 0, 2, a)
@@ -157,27 +155,17 @@ def tile_picked_trilin_none_e_kernel(tc, xT, w1, w2, w3, w4, offs, out):
         first = [first_both[:, h] for h in range(2)]
         for h in range(2):
             nc.scalar.copy(out=first[h], in_=turned(0, h))
-        product(1)
+        product(1, 1)
         a = cast_w(2, 0, 0, 2, whole_v)
         b = cast_w(2, 0, 2, 4, whole_s)
         quantise_w(2, 0, 0, 2, a)
-        idle = psum.tile([P, 512], F32, name="idle", tag="acc0")
-        for rep in range(3):
-            nc.tensor.matmul_mx(
-                out=idle[:],
-                lhsT=w_words[2, 0, 1].bitcast(FP8X4),
-                lhsT_scale=w_scales[2, 0, 1],
-                rhs=picked_words[0][:, 0:512].bitcast(FP8X4),
-                rhs_scale=picked_scales[:, 0:512],
-                start=True,
-                stop=True,
-            )
         pair = [
             keep.tile([P, HALF, PACK], F32, name="pair0", tag="w_bf2_0_0", align_bytes=64),
             None,
         ]
         nc.vector.tensor_tensor(pair[0][:], turned(1, 0), first[0], MULT)
         quantise_w(2, 0, 2, 4, b)
+        product(2, 0)
 
         g0 = cast_w(2, 1, 0, 1, whole_v)
         g1 = cast_w(2, 1, 1, 2, whole_v)
@@ -189,35 +177,36 @@ def tile_picked_trilin_none_e_kernel(tc, xT, w1, w2, w3, w4, offs, out):
         quantise_w(2, 1, 3, 4, g3)
         pair[1] = keep.tile([P, HALF, PACK], F32, name="pair1", tag="w_bf2_1_3", align_bytes=64)
         nc.vector.tensor_tensor(pair[1][:], turned(1, 1), first[1], MULT)
-        product(2)
+        product(2, 1)
 
-        w4_bf = keep.tile([P, N, PACK], BF16, name="w4_bf", align_bytes=64)
+        joint = keep.tile([P, N + HALF, PACK], BF16, name="joint", align_bytes=64)
         nc.scalar.copy(
-            out=w4_bf[:].rearrange("p (c r) t -> p c t r", r=RUN),
+            out=joint[:, :N].rearrange("p (c r) t -> p c t r", r=RUN),
             in_=w4_raw[:].rearrange("p t (c r) -> p c t r", r=RUN),
         )
-        z = [keep.tile([P, HALF, PACK], BF16, name="z%d" % h, align_bytes=64) for h in range(2)]
-        for h in range(2):
-            nc.vector.tensor_tensor(z[h][:], turned(2, h), pair[h][:], MULT)
-        w4_words = keep.tile([P, N], U32, name="w4_words", tag="w_bf2_0_0", align_bytes=64)
-        w4_scales = keep.tile([P, N], U8, name="w4_scales", align_bytes=64)
+        z_last = keep.tile([P, HALF, PACK], BF16, name="z_last", align_bytes=64)
+        nc.vector.tensor_tensor(joint[:, N:], turned(2, 0), pair[0][:], MULT)
+        nc.vector.tensor_tensor(z_last[:], turned(2, 1), pair[1][:], MULT)
+        joint_words = keep.tile([P, N + HALF], U32, name="joint_words", align_bytes=64)
+        joint_scales = keep.tile([P, N + HALF], U8, name="joint_scales", align_bytes=64)
         nc.vector.quantize_mx(
-            out=w4_words[:].bitcast(FP8X4), scales=w4_scales[:], in_=w4_bf[:].rearrange("p n t -> p (n t)")
+            out=joint_words[:].bitcast(FP8X4), scales=joint_scales[:], in_=joint[:].rearrange("p n t -> p (n t)")
         )
-
+        last_words = keep.tile([P, HALF], U32, name="last_words", align_bytes=64)
+        last_scales = keep.tile([P, HALF], U8, name="last_scales", align_bytes=64)
+        nc.vector.quantize_mx(
+            out=last_words[:].bitcast(FP8X4), scales=last_scales[:], in_=z_last[:].rearrange("p v t -> p (v t)")
+        )
+        z_words = [joint_words[:, N:], last_words[:]]
+        z_scales = [joint_scales[:, N:], last_scales[:]]
         for h in range(2):
-            z_words = keep.tile([P, HALF], U32, name="z_words%d" % h, align_bytes=64)
-            z_scales = keep.tile([P, HALF], U8, name="z_scales%d" % h, align_bytes=64)
-            nc.vector.quantize_mx(
-                out=z_words[:].bitcast(FP8X4), scales=z_scales[:], in_=z[h][:].rearrange("p v t -> p (v t)")
-            )
             acc = psum.tile([P, HALF], F32, name="acc%d" % h, tag="acc%d" % h)
             nc.tensor.matmul_mx(
                 out=acc[:],
-                lhsT=w4_words[:].bitcast(FP8X4),
-                lhsT_scale=w4_scales[:],
-                rhs=z_words[:].bitcast(FP8X4),
-                rhs_scale=z_scales[:],
+                lhsT=joint_words[:, :N].bitcast(FP8X4),
+                lhsT_scale=joint_scales[:, :N],
+                rhs=z_words[h].bitcast(FP8X4),
+                rhs_scale=z_scales[h],
                 start=True,
                 stop=True,
             )

@@ -17,20 +17,17 @@ P = 128
 PACK = 4
 K_PASS = P * PACK
 PASSES = K // K_PASS
+FACTORS = 3
 RUN = 4
-HALF = 128
-X_PIECES = ((0, 0, 512, 512), (0, 512, 1024, 128), (1, 0, 512, 512), (1, 512, 1024, 128))
+HALF = V // 2
+X_HALF = T // 2
+SCALE_ROWS = 4
+X_VECTOR_EXTRA = 128
 
 
 def tile_picked_trilin_none_e_kernel(tc, xT, w1, w2, w3, w4, offs, out):
     nc = tc.nc
     weights = (w1, w2, w3)
-
-    def cast(engine, dst, src):
-        if engine == "vector":
-            nc.vector.tensor_copy(out=dst, in_=src)
-        else:
-            nc.scalar.copy(out=dst, in_=src)
 
     with ExitStack() as ctx:
         keep = ctx.enter_context(tc.tile_pool(name="keep", bufs=1))
@@ -38,7 +35,11 @@ def tile_picked_trilin_none_e_kernel(tc, xT, w1, w2, w3, w4, offs, out):
 
         offsets = keep.tile([P, S // 16], U16, name="offsets")
         x_raw = [keep.tile([P, PACK, T], F32, name="x_raw%d" % g) for g in range(PASSES)]
-        w_raw = {(d, g): keep.tile([P, PACK, H], F32, name="w_raw%d_%d" % (d, g), tag="w_raw%d_%d" % (d, g)) for d in range(3) for g in range(PASSES)}
+        w_raw = {
+            (d, g): keep.tile([P, PACK, H], F32, name="w_raw%d_%d" % (d, g), tag="w_raw%d_%d" % (d, g))
+            for d in range(FACTORS)
+            for g in range(PASSES)
+        }
         w4_raw = keep.tile([P, PACK, N], F32, name="w4_raw")
 
         def pass_rows(matrix, g):
@@ -47,7 +48,7 @@ def tile_picked_trilin_none_e_kernel(tc, xT, w1, w2, w3, w4, offs, out):
         nc.sync.dma_start(out=x_raw[0][:], in_=pass_rows(xT, 0))
         nc.sync.dma_start(offsets[:], offs)
         nc.sync.dma_start(out=x_raw[1][:], in_=pass_rows(xT, 1))
-        for d in range(3):
+        for d in range(FACTORS):
             for g in range(PASSES):
                 nc.sync.dma_start(out=w_raw[d, g][:], in_=pass_rows(weights[d], g))
         w4_dealt = w4.rearrange("(u t q) n -> q u t n", t=PACK, q=RUN)
@@ -59,124 +60,104 @@ def tile_picked_trilin_none_e_kernel(tc, xT, w1, w2, w3, w4, offs, out):
         picked_words = []
         for g in range(PASSES):
             x_words = keep.tile([P, T], U32, name="x_words%d" % g, align_bytes=64)
-            for piece_pass, c0, c1, share in X_PIECES:
-                if piece_pass != g:
-                    continue
-                x_bf = keep.tile([P, c1 - c0, PACK], BF16, name="x_bf%d_%d" % (g, c0), align_bytes=64)
+            for c0, on_vector in ((0, X_HALF), (X_HALF, X_VECTOR_EXTRA)):
+                cols = slice(c0, c0 + X_HALF)
+                x_bf = keep.tile([P, X_HALF, PACK], BF16, name="x_bf%d_%d" % (g, c0), align_bytes=64)
                 dst = x_bf[:].rearrange("p (c r) j -> p c j r", r=RUN)
-                src = x_raw[g][:, :, c0:c1].rearrange("p j (c r) -> p c j r", r=RUN)
-                split = share // RUN
-                if share > 0:
-                    cast("vector", dst[:, :split], src[:, :split])
-                if share < c1 - c0:
-                    cast("scalar", dst[:, split:], src[:, split:])
+                src = x_raw[g][:, :, cols].rearrange("p j (c r) -> p c j r", r=RUN)
+                split = on_vector // RUN
+                nc.vector.tensor_copy(out=dst[:, :split], in_=src[:, :split])
+                if on_vector < X_HALF:
+                    nc.scalar.copy(out=dst[:, split:], in_=src[:, split:])
                 nc.vector.quantize_mx(
-                    out=x_words[:, c0:c1].bitcast(FP8X4),
-                    scales=x_scales[4 * g : P, c0:c1],
+                    out=x_words[:, cols].bitcast(FP8X4),
+                    scales=x_scales[SCALE_ROWS * g : P, cols],
                     in_=x_bf[:].rearrange("p c j -> p (c j)"),
                 )
-            words = keep.tile([P, S], U32, name="picked_words%d" % g, align_bytes=64)
-            nc.vector.tensor_copy(words[:], x_words[:].indirect(offsets[:]))
-            picked_words.append(words)
+            picked = keep.tile([P, S], U32, name="picked_words%d" % g, align_bytes=64)
+            nc.vector.tensor_copy(picked[:], x_words[:].indirect(offsets[:]))
+            picked_words.append(picked)
         picked_scales = keep.tile([P, S], U8, name="picked_scales", align_bytes=64)
         nc.vector.tensor_copy(picked_scales[:], x_scales[:].indirect(offsets[:]))
 
         w_words = {}
         w_scales = {}
 
-        def cast_w(d, g, t0, t1, parts):
-            nt = t1 - t0
-            grouped = keep.tile([P, nt, P, PACK], BF16, name="w_bf%d_%d_%d" % (d, g, t0), tag="w_bf%d_%d_%d" % (d, g, t0), align_bytes=64)
-            dst = grouped[:].rearrange("p t (u q) j -> p t u j q", q=RUN)
+        def round_w(copy, d, g, t0, t1):
+            name = "w_bf%d_%d_%d" % (d, g, t0)
+            rounded = keep.tile([P, t1 - t0, P, PACK], BF16, name=name, tag=name, align_bytes=64)
+            dst = rounded[:].rearrange("p t (u q) j -> p t u j q", q=RUN)
             src = w_raw[d, g][:].rearrange("p j (u t q) -> p t u j q", t=PACK, q=RUN)
-            for engine, u0, u1 in parts:
-                cast(engine, dst[:, :, u0:u1, :, :], src[:, t0:t1, u0:u1, :, :])
-            return grouped
+            copy(out=dst, in_=src[:, t0:t1])
+            return rounded
 
-        def quantise_w(d, g, t0, t1, grouped):
-            nt = t1 - t0
-            words = keep.tile([P, nt * P], U32, name="w_words%d_%d_%d" % (d, g, t0), align_bytes=64)
-            scales = keep.tile([P, nt * P], U8, name="w_scales%d_%d_%d" % (d, g, t0), align_bytes=64)
+        def quantise_w(d, g, t0, t1, rounded):
+            words = keep.tile([P, (t1 - t0) * P], U32, name="w_words%d_%d_%d" % (d, g, t0), align_bytes=64)
+            scales = keep.tile([P, (t1 - t0) * P], U8, name="w_scales%d_%d_%d" % (d, g, t0), align_bytes=64)
             nc.vector.quantize_mx(
-                out=words[:].bitcast(FP8X4), scales=scales[:], in_=grouped[:].rearrange("p t m j -> p (t m j)")
+                out=words[:].bitcast(FP8X4), scales=scales[:], in_=rounded[:].rearrange("p t m j -> p (t m j)")
             )
             for t in range(t0, t1):
                 cols = slice((t - t0) * P, (t - t0 + 1) * P)
                 w_words[d, g, t] = words[:, cols]
                 w_scales[d, g, t] = scales[:, cols]
 
-        banks = {(d, h): psum.tile([P, PACK, HALF], F32, name="bank%d_%d" % (d, h)) for d in range(3) for h in range(2)}
+        banks = {
+            (d, h): psum.tile([P, PACK, HALF], F32, name="bank%d_%d" % (d, h)) for d in range(FACTORS) for h in range(2)
+        }
 
         def product(d, g):
             for t in range(PACK):
                 for h in range(2):
                     cols = slice(d * V + h * HALF, d * V + (h + 1) * HALF)
-                    if True:
-                        nc.tensor.matmul_mx(
-                            out=banks[d, h][:, t, :],
-                            lhsT=w_words[d, g, t].bitcast(FP8X4),
-                            lhsT_scale=w_scales[d, g, t],
-                            rhs=picked_words[g][:, cols].bitcast(FP8X4),
-                            rhs_scale=picked_scales[4 * g : P, cols],
-                            start=(g == 0 and t == 0),
-                            stop=(g == PASSES - 1 and t == PACK - 1),
-                        )
+                    nc.tensor.matmul_mx(
+                        out=banks[d, h][:, t, :],
+                        lhsT=w_words[d, g, t].bitcast(FP8X4),
+                        lhsT_scale=w_scales[d, g, t],
+                        rhs=picked_words[g][:, cols].bitcast(FP8X4),
+                        rhs_scale=picked_scales[SCALE_ROWS * g : P, cols],
+                        start=(g == 0 and t == 0),
+                        stop=(g == PASSES - 1 and t == PACK - 1),
+                    )
 
-        def turned(d, h):
+        def by_triple(d, h):
             return banks[d, h][:].rearrange("p t v -> p v t")
 
-        U = P // RUN
-        whole_s = [("scalar", 0, U)]
-        whole_v = [("vector", 0, U)]
+        on_vector_engine = nc.vector.tensor_copy
+        on_scalar_engine = nc.scalar.copy
 
-        def cast_shared(d, g, n_vector):
-            grouped = keep.tile([P, PACK, P, PACK], BF16, name="w_bf%d_%d" % (d, g), align_bytes=64)
-            dst = grouped[:].rearrange("p t (u q) j -> p t u j q", q=RUN)
-            src = w_raw[d, g][:].rearrange("p j (u t q) -> p t u j q", t=PACK, q=RUN)
-            if n_vector:
-                cast("vector", dst[:, :n_vector], src[:, :n_vector])
-            cast("scalar", dst[:, n_vector:], src[:, n_vector:])
-            return grouped
+        for g in range(PASSES):
+            quantise_w(0, g, 0, PACK, round_w(on_scalar_engine, 0, g, 0, PACK))
+            product(0, g)
 
-        quantise_w(0, 0, 0, 4, cast_shared(0, 0, 0))
-        product(0, 0)
-        quantise_w(0, 1, 0, 4, cast_shared(0, 1, 0))
-        product(0, 1)
-        a = cast_w(1, 0, 0, 2, whole_v)
-        b = cast_w(1, 0, 2, 4, whole_s)
-        quantise_w(1, 0, 2, 4, b)
-        quantise_w(1, 0, 0, 2, a)
+        low = round_w(on_vector_engine, 1, 0, 0, 2)
+        high = round_w(on_scalar_engine, 1, 0, 2, PACK)
+        quantise_w(1, 0, 2, PACK, high)
+        quantise_w(1, 0, 0, 2, low)
         product(1, 0)
-        a = cast_w(1, 1, 0, 2, whole_v)
-        b = cast_w(1, 1, 2, 4, whole_s)
-        quantise_w(1, 1, 0, 2, a)
-        quantise_w(1, 1, 2, 4, b)
-        first_both = keep.tile([P, 2, HALF, PACK], F32, name="first", tag="w_raw1_1")
-        first = [first_both[:, h] for h in range(2)]
+        low = round_w(on_vector_engine, 1, 1, 0, 2)
+        high = round_w(on_scalar_engine, 1, 1, 2, PACK)
+        quantise_w(1, 1, 0, 2, low)
+        quantise_w(1, 1, 2, PACK, high)
+
+        first = keep.tile([P, 2, HALF, PACK], F32, name="first", tag="w_raw1_1")
         for h in range(2):
-            nc.scalar.copy(out=first[h], in_=turned(0, h))
+            nc.scalar.copy(out=first[:, h], in_=by_triple(0, h))
         product(1, 1)
-        a = cast_w(2, 0, 0, 2, whole_v)
-        b = cast_w(2, 0, 2, 4, whole_s)
-        quantise_w(2, 0, 0, 2, a)
-        pair = [
-            keep.tile([P, HALF, PACK], F32, name="pair0", tag="w_bf2_0_0", align_bytes=64),
-            None,
-        ]
-        nc.vector.tensor_tensor(pair[0][:], turned(1, 0), first[0], MULT)
-        quantise_w(2, 0, 2, 4, b)
+
+        low = round_w(on_vector_engine, 2, 0, 0, 2)
+        high = round_w(on_scalar_engine, 2, 0, 2, PACK)
+        quantise_w(2, 0, 0, 2, low)
+        pair_first = keep.tile([P, HALF, PACK], F32, name="pair0", tag="w_bf2_0_0", align_bytes=64)
+        nc.vector.tensor_tensor(pair_first[:], by_triple(1, 0), first[:, 0], MULT)
+        quantise_w(2, 0, 2, PACK, high)
         product(2, 0)
 
-        g0 = cast_w(2, 1, 0, 1, whole_v)
-        g1 = cast_w(2, 1, 1, 2, whole_v)
-        g2 = cast_w(2, 1, 2, 3, whole_s)
-        g3 = cast_w(2, 1, 3, 4, whole_s)
-        quantise_w(2, 1, 0, 1, g0)
-        quantise_w(2, 1, 1, 2, g1)
-        quantise_w(2, 1, 2, 3, g2)
-        quantise_w(2, 1, 3, 4, g3)
-        pair[1] = keep.tile([P, HALF, PACK], F32, name="pair1", tag="w_bf2_1_3", align_bytes=64)
-        nc.vector.tensor_tensor(pair[1][:], turned(1, 1), first[1], MULT)
+        rounded = [round_w(on_vector_engine if t < 2 else on_scalar_engine, 2, 1, t, t + 1) for t in range(PACK)]
+        for t in range(PACK):
+            quantise_w(2, 1, t, t + 1, rounded[t])
+        pair_second = keep.tile([P, HALF, PACK], F32, name="pair1", tag="w_bf2_1_3", align_bytes=64)
+        nc.vector.tensor_tensor(pair_second[:], by_triple(1, 1), first[:, 1], MULT)
         product(2, 1)
 
         joint = keep.tile([P, N + HALF, PACK], BF16, name="joint", align_bytes=64)
@@ -184,23 +165,24 @@ def tile_picked_trilin_none_e_kernel(tc, xT, w1, w2, w3, w4, offs, out):
             out=joint[:, :N].rearrange("p (c r) t -> p c t r", r=RUN),
             in_=w4_raw[:].rearrange("p t (c r) -> p c t r", r=RUN),
         )
-        z_last = keep.tile([P, HALF, PACK], BF16, name="z_last", align_bytes=64)
-        nc.vector.tensor_tensor(joint[:, N:], turned(2, 0), pair[0][:], MULT)
-        nc.vector.tensor_tensor(z_last[:], turned(2, 1), pair[1][:], MULT)
+        z_second = keep.tile([P, HALF, PACK], BF16, name="z_second", align_bytes=64)
+        nc.vector.tensor_tensor(joint[:, N:], by_triple(2, 0), pair_first[:], MULT)
+        nc.vector.tensor_tensor(z_second[:], by_triple(2, 1), pair_second[:], MULT)
         joint_words = keep.tile([P, N + HALF], U32, name="joint_words", align_bytes=64)
         joint_scales = keep.tile([P, N + HALF], U8, name="joint_scales", align_bytes=64)
         nc.vector.quantize_mx(
             out=joint_words[:].bitcast(FP8X4), scales=joint_scales[:], in_=joint[:].rearrange("p n t -> p (n t)")
         )
-        last_words = keep.tile([P, HALF], U32, name="last_words", align_bytes=64)
-        last_scales = keep.tile([P, HALF], U8, name="last_scales", align_bytes=64)
+        second_words = keep.tile([P, HALF], U32, name="second_words", align_bytes=64)
+        second_scales = keep.tile([P, HALF], U8, name="second_scales", align_bytes=64)
         nc.vector.quantize_mx(
-            out=last_words[:].bitcast(FP8X4), scales=last_scales[:], in_=z_last[:].rearrange("p v t -> p (v t)")
+            out=second_words[:].bitcast(FP8X4), scales=second_scales[:], in_=z_second[:].rearrange("p v t -> p (v t)")
         )
-        z_words = [joint_words[:, N:], last_words[:]]
-        z_scales = [joint_scales[:, N:], last_scales[:]]
+        z_words = (joint_words[:, N:], second_words[:])
+        z_scales = (joint_scales[:, N:], second_scales[:])
+        store_queues = (nc.sync, nc.scalar)
         for h in range(2):
-            acc = psum.tile([P, HALF], F32, name="acc%d" % h, tag="acc%d" % h)
+            acc = psum.tile([P, HALF], F32, name="acc%d" % h)
             nc.tensor.matmul_mx(
                 out=acc[:],
                 lhsT=joint_words[:, :N].bitcast(FP8X4),
@@ -212,4 +194,4 @@ def tile_picked_trilin_none_e_kernel(tc, xT, w1, w2, w3, w4, offs, out):
             )
             result = keep.tile([P, HALF], F32, name="result%d" % h)
             nc.scalar.copy(out=result[:], in_=acc[:])
-            nc.sync.dma_start(out=out[:, h * HALF : (h + 1) * HALF], in_=result[:])
+            store_queues[h].dma_start(out=out[:, h * HALF : (h + 1) * HALF], in_=result[:])

@@ -23,6 +23,8 @@ HALF = V // 2
 X_HALF = T // 2
 SCALE_ROWS = 4
 X_VECTOR_EXTRA = 128
+LAST = (FACTORS - 1, PASSES - 1)
+EARLY_COLS = 192
 
 
 def tile_picked_trilin_none_e_kernel(tc, xT, w1, w2, w3, w4, offs, out):
@@ -40,7 +42,7 @@ def tile_picked_trilin_none_e_kernel(tc, xT, w1, w2, w3, w4, offs, out):
             for d in range(FACTORS)
             for g in range(PASSES)
         }
-        w4_raw = keep.tile([P, PACK, N], F32, name="w4_raw")
+        w4_raw = keep.tile([P, PACK, N], F32, name="w4_raw", tag="w4_raw", align_bytes=64)
 
         def pass_rows(matrix, g):
             return matrix[g * K_PASS : (g + 1) * K_PASS, :].rearrange("(p j) c -> p j c", j=PACK)
@@ -50,7 +52,13 @@ def tile_picked_trilin_none_e_kernel(tc, xT, w1, w2, w3, w4, offs, out):
         nc.sync.dma_start(out=x_raw[1][:], in_=pass_rows(xT, 1))
         for d in range(FACTORS):
             for g in range(PASSES):
-                nc.sync.dma_start(out=w_raw[d, g][:], in_=pass_rows(weights[d], g))
+                if (d, g) != LAST:
+                    nc.sync.dma_start(out=w_raw[d, g][:], in_=pass_rows(weights[d], g))
+        cut = (PACK - 1) * H + EARLY_COLS
+        run_in_sbuf = w_raw[LAST][:].rearrange("p j c -> p (j c)")
+        run_in_hbm = pass_rows(w3, PASSES - 1).rearrange("p j c -> p (j c)")
+        nc.sync.dma_start(out=run_in_sbuf[:, :cut], in_=run_in_hbm[:, :cut])
+        nc.sync.dma_start(out=run_in_sbuf[:, cut:], in_=run_in_hbm[:, cut:])
         w4_dealt = w4.rearrange("(u t q) n -> q u t n", t=PACK, q=RUN)
         for q in range(RUN):
             nc.sync.dma_start(out=w4_raw[q:P:RUN, :, :], in_=w4_dealt[q])
@@ -95,7 +103,7 @@ def tile_picked_trilin_none_e_kernel(tc, xT, w1, w2, w3, w4, offs, out):
             words = keep.tile([P, (t1 - t0) * P], U32, name="w_words%d_%d_%d" % (d, g, t0), align_bytes=64)
             scales = keep.tile([P, (t1 - t0) * P], U8, name="w_scales%d_%d_%d" % (d, g, t0), align_bytes=64)
             nc.vector.quantize_mx(
-                out=words[:].bitcast(FP8X4), scales=scales[:], in_=rounded[:].rearrange("p t m j -> p (t m j)")
+                out=words[:].bitcast(FP8X4), scales=scales[:], in_=rounded[:, :].rearrange("p t m j -> p (t m j)")
             )
             for t in range(t0, t1):
                 cols = slice((t - t0) * P, (t - t0 + 1) * P)
@@ -103,7 +111,9 @@ def tile_picked_trilin_none_e_kernel(tc, xT, w1, w2, w3, w4, offs, out):
                 w_scales[d, g, t] = scales[:, cols]
 
         banks = {
-            (d, h): psum.tile([P, PACK, HALF], F32, name="bank%d_%d" % (d, h)) for d in range(FACTORS) for h in range(2)
+            (d, h): psum.tile([P, PACK, HALF], F32, name="bank%d_%d" % (d, h), tag="bank%d_%d" % (d, h))
+            for d in range(FACTORS)
+            for h in range(2)
         }
 
         def product(d, g):
@@ -145,20 +155,48 @@ def tile_picked_trilin_none_e_kernel(tc, xT, w1, w2, w3, w4, offs, out):
             nc.scalar.copy(out=first[:, h], in_=by_triple(0, h))
         product(1, 1)
 
-        low = round_w(on_vector_engine, 2, 0, 0, 2)
+        low = [round_w(on_vector_engine, 2, 0, t, t + 1) for t in range(2)]
         high = round_w(on_scalar_engine, 2, 0, 2, PACK)
-        quantise_w(2, 0, 0, 2, low)
+        for t in range(2):
+            quantise_w(2, 0, t, t + 1, low[t])
         pair_first = keep.tile([P, HALF, PACK], F32, name="pair0", tag="w_bf2_0_0", align_bytes=64)
         nc.vector.tensor_tensor(pair_first[:], by_triple(1, 0), first[:, 0], MULT)
         quantise_w(2, 0, 2, PACK, high)
         product(2, 0)
 
-        rounded = [round_w(on_vector_engine if t < 2 else on_scalar_engine, 2, 1, t, t + 1) for t in range(PACK)]
+        unread = psum.tile([P, PACK * HALF], F32, name="unread", tag="bank0_0")
+
+        def warm_up(g, t, width):
+            nc.tensor.matmul_mx(
+                out=unread[:, :width],
+                lhsT=w_words[2, g, t].bitcast(FP8X4),
+                lhsT_scale=w_scales[2, g, t],
+                rhs=picked_words[0][:, :width].bitcast(FP8X4),
+                rhs_scale=picked_scales[:, :width],
+                start=True,
+                stop=True,
+            )
+
+        warm_up(0, 1, V)
+
+        rounded = [
+            keep.tile([P, 2, P, PACK], BF16, name="w_bf2_1_%d" % t0, tag="w_bf2_1_%d" % t0, align_bytes=64)
+            for t0 in (0, 2)
+        ]
+        src = w_raw[LAST][:].rearrange("p j (u t q) -> p t u j q", t=PACK, q=RUN)
+        dst = [tile[:].rearrange("p t (u q) j -> p t u j q", q=RUN) for tile in rounded]
+        early = EARLY_COLS // (PACK * RUN)
+        for i, copy in enumerate((on_vector_engine, on_scalar_engine)):
+            copy(out=dst[i][:, :, :early], in_=src[:, 2 * i : 2 * i + 2, :early])
+            for t in range(2):
+                copy(out=dst[i][:, t, early:], in_=src[:, 2 * i + t, early:])
         for t in range(PACK):
-            quantise_w(2, 1, t, t + 1, rounded[t])
-        pair_second = keep.tile([P, HALF, PACK], F32, name="pair1", tag="w_bf2_1_3", align_bytes=64)
+            quantise_w(2, 1, t, t + 1, rounded[t // 2][:, t % 2 : t % 2 + 1])
+        pair_second = keep.tile([P, HALF, PACK], F32, name="pair1", tag="w_bf2_1_2", align_bytes=64)
         nc.vector.tensor_tensor(pair_second[:], by_triple(1, 1), first[:, 1], MULT)
         product(2, 1)
+        for t in (PACK - 1, PACK - 1):
+            warm_up(1, t, 2 * V)
 
         joint = keep.tile([P, N + HALF, PACK], BF16, name="joint", align_bytes=64)
         nc.scalar.copy(
@@ -173,7 +211,7 @@ def tile_picked_trilin_none_e_kernel(tc, xT, w1, w2, w3, w4, offs, out):
         nc.vector.quantize_mx(
             out=joint_words[:].bitcast(FP8X4), scales=joint_scales[:], in_=joint[:].rearrange("p n t -> p (n t)")
         )
-        second_words = keep.tile([P, HALF], U32, name="second_words", align_bytes=64)
+        second_words = keep.tile([P, HALF], U32, name="second_words", tag="w4_raw", align_bytes=64)
         second_scales = keep.tile([P, HALF], U8, name="second_scales", align_bytes=64)
         nc.vector.quantize_mx(
             out=second_words[:].bitcast(FP8X4), scales=second_scales[:], in_=z_second[:].rearrange("p v t -> p (v t)")

@@ -179,19 +179,21 @@ def tile_picked_trilin_none_e_kernel(tc, xT, w1, w2, w3, w4, offs, out):
 
         warm_up(0, 1, V)
 
-        rounded = [
-            keep.tile([P, 2, P, PACK], BF16, name="w_bf2_1_%d" % t0, tag="w_bf2_1_%d" % t0, align_bytes=64)
-            for t0 in (0, 2)
-        ]
+        groups = ((0, 2, on_vector_engine), (2, 3, on_scalar_engine), (3, PACK, on_scalar_engine))
         src = w_raw[LAST][:].rearrange("p j (u t q) -> p t u j q", t=PACK, q=RUN)
-        dst = [tile[:].rearrange("p t (u q) j -> p t u j q", q=RUN) for tile in rounded]
         early = EARLY_COLS // (PACK * RUN)
-        for i, copy in enumerate((on_vector_engine, on_scalar_engine)):
-            copy(out=dst[i][:, :, :early], in_=src[:, 2 * i : 2 * i + 2, :early])
-            for t in range(2):
-                copy(out=dst[i][:, t, early:], in_=src[:, 2 * i + t, early:])
+        rounded = {}
+        for t0, t1, copy in groups:
+            name = "w_bf2_1_%d" % t0
+            tile = keep.tile([P, t1 - t0, P, PACK], BF16, name=name, tag=name, align_bytes=64)
+            copy(out=tile[:].rearrange("p t (u q) j -> p t u j q", q=RUN)[:, :, :early], in_=src[:, t0:t1, :early])
+            for t in range(t0, t1):
+                rounded[t] = tile[:, t - t0 : t - t0 + 1]
+        for t0, t1, copy in groups:
+            for t in range(t0, t1):
+                copy(out=rounded[t].rearrange("p t (u q) j -> p t u j q", q=RUN)[:, :, early:], in_=src[:, t : t + 1, early:])
         for t in range(PACK):
-            quantise_w(2, 1, t, t + 1, rounded[t // 2][:, t % 2 : t % 2 + 1])
+            quantise_w(2, 1, t, t + 1, rounded[t])
         pair_second = keep.tile([P, HALF, PACK], F32, name="pair1", tag="w_bf2_1_2", align_bytes=64)
         nc.vector.tensor_tensor(pair_second[:], by_triple(1, 1), first[:, 1], MULT)
         product(2, 1)

@@ -24,7 +24,7 @@ X_HALF = T // 2
 SCALE_ROWS = 4
 X_VECTOR_EXTRA = 128
 LAST = (FACTORS - 1, PASSES - 1)
-EARLY_COLS = 192
+EARLY_COLS = 256
 
 
 def tile_picked_trilin_none_e_kernel(tc, xT, w1, w2, w3, w4, offs, out):
@@ -179,19 +179,23 @@ def tile_picked_trilin_none_e_kernel(tc, xT, w1, w2, w3, w4, offs, out):
 
         warm_up(0, 1, V)
 
-        groups = ((0, 2, on_vector_engine), (2, 3, on_scalar_engine), (3, PACK, on_scalar_engine))
+        groups = (
+            (0, 2, on_vector_engine, on_vector_engine),
+            (2, 3, on_vector_engine, on_scalar_engine),
+            (3, PACK, on_scalar_engine, on_scalar_engine),
+        )
         src = w_raw[LAST][:].rearrange("p j (u t q) -> p t u j q", t=PACK, q=RUN)
         early = EARLY_COLS // (PACK * RUN)
         rounded = {}
-        for t0, t1, copy in groups:
+        for t0, t1, copy, late_copy in groups:
             name = "w_bf2_1_%d" % t0
             tile = keep.tile([P, t1 - t0, P, PACK], BF16, name=name, tag=name, align_bytes=64)
             copy(out=tile[:].rearrange("p t (u q) j -> p t u j q", q=RUN)[:, :, :early], in_=src[:, t0:t1, :early])
             for t in range(t0, t1):
                 rounded[t] = tile[:, t - t0 : t - t0 + 1]
-        for t0, t1, copy in groups:
+        for t0, t1, copy, late_copy in groups:
             for t in range(t0, t1):
-                copy(out=rounded[t].rearrange("p t (u q) j -> p t u j q", q=RUN)[:, :, early:], in_=src[:, t : t + 1, early:])
+                late_copy(out=rounded[t].rearrange("p t (u q) j -> p t u j q", q=RUN)[:, :, early:], in_=src[:, t : t + 1, early:])
         for t in range(PACK):
             quantise_w(2, 1, t, t + 1, rounded[t])
         pair_second = keep.tile([P, HALF, PACK], F32, name="pair1", tag="w_bf2_1_2", align_bytes=64)

@@ -25,6 +25,7 @@ SCALE_ROWS = 4
 X_VECTOR_EXTRA = 128
 LAST = (FACTORS - 1, PASSES - 1)
 EARLY_COLS = 256
+SCALAR_COLS = 128
 
 
 def tile_picked_trilin_none_e_kernel(tc, xT, w1, w2, w3, w4, offs, out):
@@ -38,10 +39,14 @@ def tile_picked_trilin_none_e_kernel(tc, xT, w1, w2, w3, w4, offs, out):
         offsets = keep.tile([P, S // 16], U16, name="offsets")
         x_raw = [keep.tile([P, PACK, T], F32, name="x_raw%d" % g) for g in range(PASSES)]
         w_raw = {
-            (d, g): keep.tile([P, PACK, H], F32, name="w_raw%d_%d" % (d, g), tag="w_raw%d_%d" % (d, g))
+            (d, g): keep.tile([P, PACK, H], F32, name="w_raw%d_%d" % (d, g))[:]
             for d in range(FACTORS)
             for g in range(PASSES)
+            if (d, g) != (1, 1)
         }
+        first_start = PACK * H - SCALAR_COLS
+        shared = keep.tile([P, first_start + PACK * V], F32, name="shared")
+        w_raw[1, 1] = shared[:, : PACK * H].rearrange("p (j c) -> p j c", j=PACK)
         w4_raw = keep.tile([P, PACK, N], F32, name="w4_raw", tag="w4_raw", align_bytes=64)
 
         def pass_rows(matrix, g):
@@ -53,9 +58,9 @@ def tile_picked_trilin_none_e_kernel(tc, xT, w1, w2, w3, w4, offs, out):
         for d in range(FACTORS):
             for g in range(PASSES):
                 if (d, g) != LAST:
-                    nc.sync.dma_start(out=w_raw[d, g][:], in_=pass_rows(weights[d], g))
+                    nc.sync.dma_start(out=w_raw[d, g], in_=pass_rows(weights[d], g))
         cut = (PACK - 1) * H + EARLY_COLS
-        run_in_sbuf = w_raw[LAST][:].rearrange("p j c -> p (j c)")
+        run_in_sbuf = w_raw[LAST].rearrange("p j c -> p (j c)")
         run_in_hbm = pass_rows(w3, PASSES - 1).rearrange("p j c -> p (j c)")
         nc.sync.dma_start(out=run_in_sbuf[:, :cut], in_=run_in_hbm[:, :cut])
         nc.sync.dma_start(out=run_in_sbuf[:, cut:], in_=run_in_hbm[:, cut:])
@@ -95,7 +100,7 @@ def tile_picked_trilin_none_e_kernel(tc, xT, w1, w2, w3, w4, offs, out):
             name = "w_bf%d_%d_%d" % (d, g, t0)
             rounded = keep.tile([P, t1 - t0, P, PACK], BF16, name=name, tag=name, align_bytes=64)
             dst = rounded[:].rearrange("p t (u q) j -> p t u j q", q=RUN)
-            src = w_raw[d, g][:].rearrange("p j (u t q) -> p t u j q", t=PACK, q=RUN)
+            src = w_raw[d, g].rearrange("p j (u t q) -> p t u j q", t=PACK, q=RUN)
             copy(out=dst, in_=src[:, t0:t1])
             return rounded
 
@@ -145,12 +150,17 @@ def tile_picked_trilin_none_e_kernel(tc, xT, w1, w2, w3, w4, offs, out):
         quantise_w(1, 0, 2, PACK, high)
         quantise_w(1, 0, 0, 2, low)
         product(1, 0)
-        low = round_w(on_vector_engine, 1, 1, 0, 2)
-        high = round_w(on_scalar_engine, 1, 1, 2, PACK)
-        quantise_w(1, 1, 0, 2, low)
-        quantise_w(1, 1, 2, PACK, high)
+        rounded = keep.tile([P, PACK, P, PACK], BF16, name="w_bf1_1", align_bytes=64)
+        dst = rounded[:].rearrange("p t (u q) j -> p t u j q", q=RUN)
+        src = w_raw[1, 1].rearrange("p j (u t q) -> p t u j q", t=PACK, q=RUN)
+        split = (H - SCALAR_COLS) // (PACK * RUN)
+        nc.scalar.copy(out=dst[:, :, split:], in_=src[:, :, split:])
+        for t0 in (0, 2):
+            nc.vector.tensor_copy(out=dst[:, t0 : t0 + 2, :split], in_=src[:, t0 : t0 + 2, :split])
+        for t0 in (0, 2):
+            quantise_w(1, 1, t0, t0 + 2, rounded[:, t0 : t0 + 2])
 
-        first = keep.tile([P, 2, HALF, PACK], F32, name="first", tag="w_raw1_1")
+        first = shared[:, first_start:].rearrange("p (v h t) -> p h v t", h=2, t=PACK)
         for h in range(2):
             nc.scalar.copy(out=first[:, h], in_=by_triple(0, h))
         product(1, 1)
@@ -184,7 +194,7 @@ def tile_picked_trilin_none_e_kernel(tc, xT, w1, w2, w3, w4, offs, out):
             (2, 3, on_vector_engine, on_scalar_engine),
             (3, PACK, on_scalar_engine, on_scalar_engine),
         )
-        src = w_raw[LAST][:].rearrange("p j (u t q) -> p t u j q", t=PACK, q=RUN)
+        src = w_raw[LAST].rearrange("p j (u t q) -> p t u j q", t=PACK, q=RUN)
         early = EARLY_COLS // (PACK * RUN)
         rounded = {}
         for t0, t1, copy, late_copy in groups:

@@ -24,7 +24,8 @@ X_HALF = T // 2
 SCALE_ROWS = 4
 X_VECTOR_EXTRA = 128
 LAST = (FACTORS - 1, PASSES - 1)
-EARLY_COLS = 256
+EARLY_COLS = 224
+THIRD_SLOT_COLS = 320
 SCALAR_COLS = 128
 
 
@@ -189,23 +190,24 @@ def tile_picked_trilin_none_e_kernel(tc, xT, w1, w2, w3, w4, offs, out):
 
         warm_up(0, 1, V)
 
-        groups = (
-            (0, 2, on_vector_engine, on_vector_engine),
-            (2, 3, on_vector_engine, on_scalar_engine),
-            (3, PACK, on_scalar_engine, on_scalar_engine),
-        )
         src = w_raw[LAST].rearrange("p j (u t q) -> p t u j q", t=PACK, q=RUN)
-        early = EARLY_COLS // (PACK * RUN)
-        rounded = {}
-        for t0, t1, copy, late_copy in groups:
-            name = "w_bf2_1_%d" % t0
-            tile = keep.tile([P, t1 - t0, P, PACK], BF16, name=name, tag=name, align_bytes=64)
-            copy(out=tile[:].rearrange("p t (u q) j -> p t u j q", q=RUN)[:, :, :early], in_=src[:, t0:t1, :early])
-            for t in range(t0, t1):
-                rounded[t] = tile[:, t - t0 : t - t0 + 1]
-        for t0, t1, copy, late_copy in groups:
-            for t in range(t0, t1):
-                late_copy(out=rounded[t].rearrange("p t (u q) j -> p t u j q", q=RUN)[:, :, early:], in_=src[:, t : t + 1, early:])
+        low = keep.tile([P, 2, P, PACK], BF16, name="w_bf2_1_0", align_bytes=64)
+        third = keep.tile([P, 1, P, PACK], BF16, name="w_bf2_1_2", tag="w_bf2_1_2", align_bytes=64)
+        fourth = keep.tile([P, 1, P, PACK], BF16, name="w_bf2_1_3", align_bytes=64)
+        rounded = (low[:, 0:1], low[:, 1:2], third[:], fourth[:])
+
+        def round_last(copy, tile, t0, t1, c0, c1):
+            groups = slice(c0 // (PACK * RUN), c1 // (PACK * RUN))
+            copy(out=tile.rearrange("p t (u q) j -> p t u j q", q=RUN)[:, :, groups], in_=src[:, t0:t1, groups])
+
+        round_last(on_vector_engine, low[:], 0, 2, 0, EARLY_COLS)
+        round_last(on_vector_engine, rounded[2], 2, 3, 0, EARLY_COLS)
+        round_last(on_scalar_engine, rounded[3], 3, 4, 0, EARLY_COLS)
+        round_last(on_vector_engine, rounded[0], 0, 1, EARLY_COLS, H)
+        round_last(on_vector_engine, rounded[1], 1, 2, EARLY_COLS, H)
+        round_last(on_vector_engine, rounded[2], 2, 3, EARLY_COLS, THIRD_SLOT_COLS)
+        round_last(on_scalar_engine, rounded[2], 2, 3, THIRD_SLOT_COLS, H)
+        round_last(on_scalar_engine, rounded[3], 3, 4, EARLY_COLS, H)
         for t in range(PACK):
             quantise_w(2, 1, t, t + 1, rounded[t])
         pair_second = keep.tile([P, HALF, PACK], F32, name="pair1", tag="w_bf2_1_2", align_bytes=64)

@@ -236,18 +236,24 @@ def tile_picked_trilin_none_e_kernel(tc, xT, w1, w2, w3, w4, offs, out):
         )
         z_words = (joint_words[:, N:], second_words[:])
         z_scales = (joint_scales[:, N:], second_scales[:])
-        store_queues = (nc.sync, nc.scalar)
-        for h in range(2):
-            acc = psum.tile([P, HALF], F32, name="acc%d" % h)
+        results = [keep.tile([P, HALF], F32, name="result%d" % h) for h in range(2)]
+        pieces = (
+            (0, 0, HALF // 2, "acc0", on_vector_engine),
+            (0, HALF // 2, HALF, "acc1", on_scalar_engine),
+            (1, 0, HALF // 2, "bank1_0", on_vector_engine),
+            (1, HALF // 2, HALF, "bank1_1", on_scalar_engine),
+        )
+        for h, c0, c1, bank, copy in pieces:
+            acc = psum.tile([P, c1 - c0], F32, name="acc%d_%d" % (h, c0), tag=bank)
             nc.tensor.matmul_mx(
                 out=acc[:],
                 lhsT=joint_words[:, :N].bitcast(FP8X4),
                 lhsT_scale=joint_scales[:, :N],
-                rhs=z_words[h].bitcast(FP8X4),
-                rhs_scale=z_scales[h],
+                rhs=z_words[h][:, c0:c1].bitcast(FP8X4),
+                rhs_scale=z_scales[h][:, c0:c1],
                 start=True,
                 stop=True,
             )
-            result = keep.tile([P, HALF], F32, name="result%d" % h)
-            nc.scalar.copy(out=result[:], in_=acc[:])
-            store_queues[h].dma_start(out=out[:, h * HALF : (h + 1) * HALF], in_=result[:])
+            copy(out=results[h][:, c0:c1], in_=acc[:])
+        for h, queue in enumerate((nc.sync, nc.scalar)):
+            queue.dma_start(out=out[:, h * HALF : (h + 1) * HALF], in_=results[h][:])

@@ -26,6 +26,7 @@ X_VECTOR_EXTRA = 128
 LAST = (FACTORS - 1, PASSES - 1)
 EARLY_COLS = 224
 THIRD_SLOT_COLS = 320
+THIRD_SLOT_EARLY = 160
 SCALAR_COLS = 128
 
 
@@ -201,8 +202,9 @@ def tile_picked_trilin_none_e_kernel(tc, xT, w1, w2, w3, w4, offs, out):
             copy(out=tile.rearrange("p t (u q) j -> p t u j q", q=RUN)[:, :, groups], in_=src[:, t0:t1, groups])
 
         round_last(on_vector_engine, low[:], 0, 2, 0, EARLY_COLS)
-        round_last(on_vector_engine, rounded[2], 2, 3, 0, EARLY_COLS)
+        round_last(on_vector_engine, rounded[2], 2, 3, 0, THIRD_SLOT_EARLY)
         round_last(on_scalar_engine, rounded[3], 3, 4, 0, EARLY_COLS)
+        round_last(on_scalar_engine, rounded[2], 2, 3, THIRD_SLOT_EARLY, EARLY_COLS)
         round_last(on_vector_engine, rounded[0], 0, 1, EARLY_COLS, H)
         round_last(on_vector_engine, rounded[1], 1, 2, EARLY_COLS, H)
         round_last(on_vector_engine, rounded[2], 2, 3, EARLY_COLS, THIRD_SLOT_COLS)

@@ -121,11 +121,12 @@ def tile_picked_trilin_none_e_kernel(tc, xT, w1, w2, w3, w4, offs, out):
             (d, h): psum.tile([P, PACK, HALF], F32, name="bank%d_%d" % (d, h), tag="bank%d_%d" % (d, h))
             for d in range(FACTORS)
             for h in range(2)
+            if (d, h) != (1, 1)
         }
 
-        def product(d, g):
+        def product(d, g, halves=(0, 1)):
             for t in range(PACK):
-                for h in range(2):
+                for h in halves:
                     cols = slice(d * V + h * HALF, d * V + (h + 1) * HALF)
                     nc.tensor.matmul_mx(
                         out=banks[d, h][:, t, :],
@@ -151,7 +152,7 @@ def tile_picked_trilin_none_e_kernel(tc, xT, w1, w2, w3, w4, offs, out):
         high = round_w(on_scalar_engine, 1, 0, 2, PACK)
         quantise_w(1, 0, 2, PACK, high)
         quantise_w(1, 0, 0, 2, low)
-        product(1, 0)
+        product(1, 0, (0,))
         rounded = keep.tile([P, PACK, P, PACK], BF16, name="w_bf1_1", align_bytes=64)
         dst = rounded[:].rearrange("p t (u q) j -> p t u j q", q=RUN)
         src = w_raw[1, 1].rearrange("p j (u t q) -> p t u j q", t=PACK, q=RUN)
@@ -165,7 +166,7 @@ def tile_picked_trilin_none_e_kernel(tc, xT, w1, w2, w3, w4, offs, out):
         first = shared[:, first_start:].rearrange("p (v h t) -> p h v t", h=2, t=PACK)
         for h in range(2):
             nc.scalar.copy(out=first[:, h], in_=by_triple(0, h))
-        product(1, 1)
+        product(1, 1, (0,))
 
         low = [round_w(on_vector_engine, 2, 0, t, t + 1) for t in range(2)]
         high = round_w(on_scalar_engine, 2, 0, 2, PACK)
@@ -176,20 +177,9 @@ def tile_picked_trilin_none_e_kernel(tc, xT, w1, w2, w3, w4, offs, out):
         quantise_w(2, 0, 2, PACK, high)
         product(2, 0)
 
-        unread = psum.tile([P, PACK * HALF], F32, name="unread", tag="bank0_0")
-
-        def warm_up(g, t, width):
-            nc.tensor.matmul_mx(
-                out=unread[:, :width],
-                lhsT=w_words[2, g, t].bitcast(FP8X4),
-                lhsT_scale=w_scales[2, g, t],
-                rhs=picked_words[0][:, :width].bitcast(FP8X4),
-                rhs_scale=picked_scales[:, :width],
-                start=True,
-                stop=True,
-            )
-
-        warm_up(0, 1, V)
+        banks[1, 1] = psum.tile([P, PACK, HALF], F32, name="bank1_1", tag="bank1_0")
+        for g in range(PASSES):
+            product(1, g, (1,))
 
         src = w_raw[LAST].rearrange("p j (u t q) -> p t u j q", t=PACK, q=RUN)
         low = keep.tile([P, 2, P, PACK], BF16, name="w_bf2_1_0", align_bytes=64)
@@ -215,8 +205,6 @@ def tile_picked_trilin_none_e_kernel(tc, xT, w1, w2, w3, w4, offs, out):
         pair_second = keep.tile([P, HALF, PACK], F32, name="pair1", tag="w_bf2_1_2", align_bytes=64)
         nc.vector.tensor_tensor(pair_second[:], by_triple(1, 1), first[:, 1], MULT)
         product(2, 1)
-        for t in (PACK - 1, PACK - 1):
-            warm_up(1, t, 2 * V)
 
         joint = keep.tile([P, N + HALF, PACK], BF16, name="joint", align_bytes=64)
         nc.scalar.copy(
@@ -242,8 +230,8 @@ def tile_picked_trilin_none_e_kernel(tc, xT, w1, w2, w3, w4, offs, out):
         pieces = (
             (0, 0, HALF // 2, "acc0", on_vector_engine),
             (0, HALF // 2, HALF, "acc1", on_scalar_engine),
-            (1, 0, HALF // 2, "bank1_0", on_vector_engine),
-            (1, HALF // 2, HALF, "bank1_1", on_scalar_engine),
+            (1, 0, HALF // 2, "bank0_0", on_vector_engine),
+            (1, HALF // 2, HALF, "bank0_1", on_scalar_engine),
         )
         for h, c0, c1, bank, copy in pieces:
             acc = psum.tile([P, c1 - c0], F32, name="acc%d_%d" % (h, c0), tag=bank)

@@ -167,6 +167,9 @@ def tile_picked_trilin_none_e_kernel(tc, xT, w1, w2, w3, w4, offs, out):
         for h in range(2):
             nc.scalar.copy(out=first[:, h], in_=by_triple(0, h))
         product(1, 1, (0,))
+        banks[1, 1] = psum.tile([P, PACK, HALF], F32, name="bank1_1", tag="bank0_1")
+        for g in range(PASSES):
+            product(1, g, (1,))
 
         low = [round_w(on_vector_engine, 2, 0, t, t + 1) for t in range(2)]
         high = round_w(on_scalar_engine, 2, 0, 2, PACK)
@@ -176,10 +179,6 @@ def tile_picked_trilin_none_e_kernel(tc, xT, w1, w2, w3, w4, offs, out):
         nc.vector.tensor_tensor(pair_first[:], by_triple(1, 0), first[:, 0], MULT)
         quantise_w(2, 0, 2, PACK, high)
         product(2, 0)
-
-        banks[1, 1] = psum.tile([P, PACK, HALF], F32, name="bank1_1", tag="bank1_0")
-        for g in range(PASSES):
-            product(1, g, (1,))
 
         src = w_raw[LAST].rearrange("p j (u t q) -> p t u j q", t=PACK, q=RUN)
         low = keep.tile([P, 2, P, PACK], BF16, name="w_bf2_1_0", align_bytes=64)
@@ -231,7 +230,7 @@ def tile_picked_trilin_none_e_kernel(tc, xT, w1, w2, w3, w4, offs, out):
             (0, 0, HALF // 2, "acc0", on_vector_engine),
             (0, HALF // 2, HALF, "acc1", on_scalar_engine),
             (1, 0, HALF // 2, "bank0_0", on_vector_engine),
-            (1, HALF // 2, HALF, "bank0_1", on_scalar_engine),
+            (1, HALF // 2, HALF, "bank1_0", on_scalar_engine),
         )
         for h, c0, c1, bank, copy in pieces:
             acc = psum.tile([P, c1 - c0], F32, name="acc%d_%d" % (h, c0), tag=bank)

@@ -28,6 +28,7 @@ EARLY_COLS = 224
 THIRD_SLOT_COLS = 320
 THIRD_SLOT_EARLY = 160
 SCALAR_COLS = 128
+DMA_ALIGN = 256
 
 
 def tile_picked_trilin_none_e_kernel(tc, xT, w1, w2, w3, w4, offs, out):
@@ -39,17 +40,17 @@ def tile_picked_trilin_none_e_kernel(tc, xT, w1, w2, w3, w4, offs, out):
         psum = ctx.enter_context(tc.psum_pool(name="psum", bufs=1))
 
         offsets = keep.tile([P, S // 16], U16, name="offsets")
-        x_raw = [keep.tile([P, PACK, T], F32, name="x_raw%d" % g) for g in range(PASSES)]
+        x_raw = [keep.tile([P, PACK, T], F32, name="x_raw%d" % g, align_bytes=DMA_ALIGN) for g in range(PASSES)]
         w_raw = {
-            (d, g): keep.tile([P, PACK, H], F32, name="w_raw%d_%d" % (d, g))[:]
+            (d, g): keep.tile([P, PACK, H], F32, name="w_raw%d_%d" % (d, g), align_bytes=DMA_ALIGN)[:]
             for d in range(FACTORS)
             for g in range(PASSES)
             if (d, g) != (1, 1)
         }
         first_start = PACK * H - SCALAR_COLS
-        shared = keep.tile([P, first_start + PACK * V], F32, name="shared")
+        shared = keep.tile([P, first_start + PACK * V], F32, name="shared", align_bytes=DMA_ALIGN)
         w_raw[1, 1] = shared[:, : PACK * H].rearrange("p (j c) -> p j c", j=PACK)
-        w4_raw = keep.tile([P, PACK, N], F32, name="w4_raw", tag="w4_raw", align_bytes=64)
+        w4_raw = keep.tile([P, PACK, N], F32, name="w4_raw", tag="w4_raw", align_bytes=DMA_ALIGN)
 
         def pass_rows(matrix, g):
             return matrix[g * K_PASS : (g + 1) * K_PASS, :].rearrange("(p j) c -> p j c", j=PACK)
@@ -218,14 +219,14 @@ def tile_picked_trilin_none_e_kernel(tc, xT, w1, w2, w3, w4, offs, out):
         nc.vector.quantize_mx(
             out=joint_words[:].bitcast(FP8X4), scales=joint_scales[:], in_=joint[:].rearrange("p n t -> p (n t)")
         )
-        second_words = keep.tile([P, HALF], U32, name="second_words", tag="w4_raw", align_bytes=64)
+        second_words = keep.tile([P, HALF], U32, name="second_words", tag="w4_raw", align_bytes=DMA_ALIGN)
         second_scales = keep.tile([P, HALF], U8, name="second_scales", align_bytes=64)
         nc.vector.quantize_mx(
             out=second_words[:].bitcast(FP8X4), scales=second_scales[:], in_=z_second[:].rearrange("p v t -> p (v t)")
         )
         z_words = (joint_words[:, N:], second_words[:])
         z_scales = (joint_scales[:, N:], second_scales[:])
-        results = [keep.tile([P, HALF], F32, name="result%d" % h) for h in range(2)]
+        results = [keep.tile([P, HALF], F32, name="result%d" % h, align_bytes=DMA_ALIGN) for h in range(2)]
         pieces = (
             (0, 0, HALF // 2, "acc0", on_vector_engine),
             (0, HALF // 2, HALF, "acc1", on_scalar_engine),

@@ -24,9 +24,9 @@ X_HALF = T // 2
 SCALE_ROWS = 4
 X_VECTOR_EXTRA = 128
 LAST = (FACTORS - 1, PASSES - 1)
-EARLY_COLS = 224
-THIRD_SLOT_COLS = 320
-THIRD_SLOT_EARLY = 160
+EARLY_COLS = 256
+THIRD_SLOT_COLS = 336
+THIRD_SLOT_EARLY = 176
 SCALAR_COLS = 128
 DMA_ALIGN = 256
 

@@ -28,6 +28,7 @@ EARLY_COLS = 256
 THIRD_SLOT_COLS = 336
 THIRD_SLOT_EARLY = 176
 SCALAR_COLS = 128
+GPSIMD_TRIPLES = 24
 DMA_ALIGN = 256
 
 
@@ -213,7 +214,11 @@ def tile_picked_trilin_none_e_kernel(tc, xT, w1, w2, w3, w4, offs, out):
         )
         z_second = keep.tile([P, HALF, PACK], BF16, name="z_second", align_bytes=64)
         nc.vector.tensor_tensor(joint[:, N:], by_triple(2, 0), pair_first[:], MULT)
-        nc.vector.tensor_tensor(z_second[:], by_triple(2, 1), pair_second[:], MULT)
+        own = HALF - GPSIMD_TRIPLES
+        third_copy = keep.tile([P, GPSIMD_TRIPLES, PACK], F32, name="third_copy", align_bytes=64)
+        nc.scalar.copy(out=third_copy[:], in_=by_triple(2, 1)[:, own:])
+        nc.gpsimd.tensor_tensor(z_second[:, own:], third_copy[:], pair_second[:, own:], MULT)
+        nc.vector.tensor_tensor(z_second[:, :own], by_triple(2, 1)[:, :own], pair_second[:, :own], MULT)
         joint_words = keep.tile([P, N + HALF], U32, name="joint_words", align_bytes=64)
         joint_scales = keep.tile([P, N + HALF], U8, name="joint_scales", align_bytes=64)
         nc.vector.quantize_mx(

@@ -43,7 +43,7 @@ def tile_picked_trilin_none_e_kernel(tc, xT, w1, w2, w3, w4, offs, out):
         offsets = keep.tile([P, S // 16], U16, name="offsets")
         x_raw = [keep.tile([P, PACK, T], F32, name="x_raw%d" % g, align_bytes=DMA_ALIGN) for g in range(PASSES)]
         w_raw = {
-            (d, g): keep.tile([P, PACK, H], F32, name="w_raw%d_%d" % (d, g), align_bytes=DMA_ALIGN)[:]
+            (d, g): keep.tile([P, PACK, H], F32, name="w_raw%d_%d" % (d, g), tag="w_raw%d_%d" % (d, g), align_bytes=DMA_ALIGN)[:]
             for d in range(FACTORS)
             for g in range(PASSES)
             if (d, g) != (1, 1)
@@ -203,7 +203,7 @@ def tile_picked_trilin_none_e_kernel(tc, xT, w1, w2, w3, w4, offs, out):
         round_last(on_scalar_engine, rounded[3], 3, 4, EARLY_COLS, H)
         for t in range(PACK):
             quantise_w(2, 1, t, t + 1, rounded[t])
-        pair_second = keep.tile([P, HALF, PACK], F32, name="pair1", tag="w_bf2_1_2", align_bytes=64)
+        pair_second = keep.tile([P, HALF, PACK], F32, name="pair1", tag="w_raw2_1", align_bytes=DMA_ALIGN)
         nc.vector.tensor_tensor(pair_second[:], by_triple(1, 1), first[:, 1], MULT)
         product(2, 1)
 
@@ -215,22 +215,25 @@ def tile_picked_trilin_none_e_kernel(tc, xT, w1, w2, w3, w4, offs, out):
         z_second = keep.tile([P, HALF, PACK], BF16, name="z_second", align_bytes=64)
         nc.vector.tensor_tensor(joint[:, N:], by_triple(2, 0), pair_first[:], MULT)
         own = HALF - GPSIMD_TRIPLES
-        third_copy = keep.tile([P, GPSIMD_TRIPLES, PACK], F32, name="third_copy", align_bytes=64)
+        third_copy = keep.tile([P, GPSIMD_TRIPLES, PACK], F32, name="third_copy", tag="third_copy", align_bytes=64)
         nc.scalar.copy(out=third_copy[:], in_=by_triple(2, 1)[:, own:])
         nc.gpsimd.tensor_tensor(z_second[:, own:], third_copy[:], pair_second[:, own:], MULT)
         nc.vector.tensor_tensor(z_second[:, :own], by_triple(2, 1)[:, :own], pair_second[:, :own], MULT)
-        joint_words = keep.tile([P, N + HALF], U32, name="joint_words", align_bytes=64)
-        joint_scales = keep.tile([P, N + HALF], U8, name="joint_scales", align_bytes=64)
-        nc.vector.quantize_mx(
-            out=joint_words[:].bitcast(FP8X4), scales=joint_scales[:], in_=joint[:].rearrange("p n t -> p (n t)")
-        )
+        w4_words = keep.tile([P, N], U32, name="w4_words", tag="third_copy", align_bytes=64)
+        w4_scales = keep.tile([P, N], U8, name="w4_scales", align_bytes=64)
+        first_words = keep.tile([P, HALF], U32, name="first_words", align_bytes=64)
+        first_scales = keep.tile([P, HALF], U8, name="first_scales", align_bytes=64)
+        for words, scales, cols in ((w4_words, w4_scales, slice(0, N)), (first_words, first_scales, slice(N, N + HALF))):
+            nc.vector.quantize_mx(
+                out=words[:].bitcast(FP8X4), scales=scales[:], in_=joint[:, cols].rearrange("p n t -> p (n t)")
+            )
         second_words = keep.tile([P, HALF], U32, name="second_words", tag="w4_raw", align_bytes=DMA_ALIGN)
         second_scales = keep.tile([P, HALF], U8, name="second_scales", align_bytes=64)
         nc.vector.quantize_mx(
             out=second_words[:].bitcast(FP8X4), scales=second_scales[:], in_=z_second[:].rearrange("p v t -> p (v t)")
         )
-        z_words = (joint_words[:, N:], second_words[:])
-        z_scales = (joint_scales[:, N:], second_scales[:])
+        z_words = (first_words[:], second_words[:])
+        z_scales = (first_scales[:], second_scales[:])
         results = [keep.tile([P, HALF], F32, name="result%d" % h, align_bytes=DMA_ALIGN) for h in range(2)]
         pieces = (
             (0, 0, HALF // 2, "acc0", on_vector_engine),
@@ -242,8 +245,8 @@ def tile_picked_trilin_none_e_kernel(tc, xT, w1, w2, w3, w4, offs, out):
             acc = psum.tile([P, c1 - c0], F32, name="acc%d_%d" % (h, c0), tag=bank)
             nc.tensor.matmul_mx(
                 out=acc[:],
-                lhsT=joint_words[:, :N].bitcast(FP8X4),
-                lhsT_scale=joint_scales[:, :N],
+                lhsT=w4_words[:].bitcast(FP8X4),
+                lhsT_scale=w4_scales[:],
                 rhs=z_words[h][:, c0:c1].bitcast(FP8X4),
                 rhs_scale=z_scales[h][:, c0:c1],
                 start=True,

from contextlib import ExitStack

import concourse.mybir as mybir

K, T, S, V, H, N = 1024, 1024, 768, 256, 512, 128
FLOPS = 2 * (3 * K * H * V + H * N * V)

F32 = mybir.dt.float32
BF16 = mybir.dt.bfloat16
U32 = mybir.dt.uint32
U16 = mybir.dt.uint16
U8 = mybir.dt.uint8
FP8X4 = mybir.dt.float8_e4m3fn_x4
MULT = mybir.AluOpType.mult

P = 128
PACK = 4
K_PASS = P * PACK
PASSES = K // K_PASS
FACTORS = 3
RUN = 4
HALF = V // 2
X_HALF = T // 2
SCALE_ROWS = 4
X_VECTOR_EXTRA = 128
LAST = (FACTORS - 1, PASSES - 1)
EARLY_COLS = 256
THIRD_SLOT_COLS = 336
THIRD_SLOT_EARLY = 176
SCALAR_COLS = 128
GPSIMD_TRIPLES = 24
DMA_ALIGN = 256


def tile_picked_trilin_none_e_kernel(tc, xT, w1, w2, w3, w4, offs, out):
    nc = tc.nc
    weights = (w1, w2, w3)

    with ExitStack() as ctx:
        keep = ctx.enter_context(tc.tile_pool(name="keep", bufs=1))
        psum = ctx.enter_context(tc.psum_pool(name="psum", bufs=1))

        offsets = keep.tile([P, S // 16], U16, name="offsets")
        x_raw = [keep.tile([P, PACK, T], F32, name="x_raw%d" % g, align_bytes=DMA_ALIGN) for g in range(PASSES)]
        w_raw = {
            (d, g): keep.tile([P, PACK, H], F32, name="w_raw%d_%d" % (d, g), tag="w_raw%d_%d" % (d, g), align_bytes=DMA_ALIGN)[:]
            for d in range(FACTORS)
            for g in range(PASSES)
            if (d, g) != (1, 1)
        }
        first_start = PACK * H - SCALAR_COLS
        shared = keep.tile([P, first_start + PACK * V], F32, name="shared", align_bytes=DMA_ALIGN)
        w_raw[1, 1] = shared[:, : PACK * H].rearrange("p (j c) -> p j c", j=PACK)
        w4_raw = keep.tile([P, PACK, N], F32, name="w4_raw", tag="w4_raw", align_bytes=DMA_ALIGN)

        def pass_rows(matrix, g):
            return matrix[g * K_PASS : (g + 1) * K_PASS, :].rearrange("(p j) c -> p j c", j=PACK)

        nc.sync.dma_start(out=x_raw[0][:], in_=pass_rows(xT, 0))
        nc.sync.dma_start(offsets[:], offs)
        nc.sync.dma_start(out=x_raw[1][:], in_=pass_rows(xT, 1))
        for d in range(FACTORS):
            for g in range(PASSES):
                if (d, g) != LAST:
                    nc.sync.dma_start(out=w_raw[d, g], in_=pass_rows(weights[d], g))
        cut = (PACK - 1) * H + EARLY_COLS
        run_in_sbuf = w_raw[LAST].rearrange("p j c -> p (j c)")
        run_in_hbm = pass_rows(w3, PASSES - 1).rearrange("p j c -> p (j c)")
        nc.sync.dma_start(out=run_in_sbuf[:, :cut], in_=run_in_hbm[:, :cut])
        nc.sync.dma_start(out=run_in_sbuf[:, cut:], in_=run_in_hbm[:, cut:])
        w4_dealt = w4.rearrange("(u t q) n -> q u t n", t=PACK, q=RUN)
        for q in range(RUN):
            nc.sync.dma_start(out=w4_raw[q:P:RUN, :, :], in_=w4_dealt[q])

        x_scales = keep.tile([P, T], U8, name="x_scales", align_bytes=64)
        nc.gpsimd.memset(x_scales[:], 0)
        picked_words = []
        for g in range(PASSES):
            x_words = keep.tile([P, T], U32, name="x_words%d" % g, align_bytes=64)
            for c0, on_vector in ((0, X_HALF), (X_HALF, X_VECTOR_EXTRA)):
                cols = slice(c0, c0 + X_HALF)
                x_bf = keep.tile([P, X_HALF, PACK], BF16, name="x_bf%d_%d" % (g, c0), align_bytes=64)
                dst = x_bf[:].rearrange("p (c r) j -> p c j r", r=RUN)
                src = x_raw[g][:, :, cols].rearrange("p j (c r) -> p c j r", r=RUN)
                split = on_vector // RUN
                nc.vector.tensor_copy(out=dst[:, :split], in_=src[:, :split])
                if on_vector < X_HALF:
                    nc.scalar.copy(out=dst[:, split:], in_=src[:, split:])
                nc.vector.quantize_mx(
                    out=x_words[:, cols].bitcast(FP8X4),
                    scales=x_scales[SCALE_ROWS * g : P, cols],
                    in_=x_bf[:].rearrange("p c j -> p (c j)"),
                )
            picked = keep.tile([P, S], U32, name="picked_words%d" % g, align_bytes=64)
            nc.vector.tensor_copy(picked[:], x_words[:].indirect(offsets[:]))
            picked_words.append(picked)
        picked_scales = keep.tile([P, S], U8, name="picked_scales", align_bytes=64)
        nc.vector.tensor_copy(picked_scales[:], x_scales[:].indirect(offsets[:]))

        w_words = {}
        w_scales = {}

        def round_w(copy, d, g, t0, t1):
            name = "w_bf%d_%d_%d" % (d, g, t0)
            rounded = keep.tile([P, t1 - t0, P, PACK], BF16, name=name, tag=name, align_bytes=64)
            dst = rounded[:].rearrange("p t (u q) j -> p t u j q", q=RUN)
            src = w_raw[d, g].rearrange("p j (u t q) -> p t u j q", t=PACK, q=RUN)
            copy(out=dst, in_=src[:, t0:t1])
            return rounded

        def quantise_w(d, g, t0, t1, rounded):
            words = keep.tile([P, (t1 - t0) * P], U32, name="w_words%d_%d_%d" % (d, g, t0), align_bytes=64)
            scales = keep.tile([P, (t1 - t0) * P], U8, name="w_scales%d_%d_%d" % (d, g, t0), align_bytes=64)
            nc.vector.quantize_mx(
                out=words[:].bitcast(FP8X4), scales=scales[:], in_=rounded[:, :].rearrange("p t m j -> p (t m j)")
            )
            for t in range(t0, t1):
                cols = slice((t - t0) * P, (t - t0 + 1) * P)
                w_words[d, g, t] = words[:, cols]
                w_scales[d, g, t] = scales[:, cols]

        banks = {
            (d, h): psum.tile([P, PACK, HALF], F32, name="bank%d_%d" % (d, h), tag="bank%d_%d" % (d, h))
            for d in range(FACTORS)
            for h in range(2)
            if (d, h) != (1, 1)
        }

        def product(d, g, halves=(0, 1)):
            for t in range(PACK):
                for h in halves:
                    cols = slice(d * V + h * HALF, d * V + (h + 1) * HALF)
                    nc.tensor.matmul_mx(
                        out=banks[d, h][:, t, :],
                        lhsT=w_words[d, g, t].bitcast(FP8X4),
                        lhsT_scale=w_scales[d, g, t],
                        rhs=picked_words[g][:, cols].bitcast(FP8X4),
                        rhs_scale=picked_scales[SCALE_ROWS * g : P, cols],
                        start=(g == 0 and t == 0),
                        stop=(g == PASSES - 1 and t == PACK - 1),
                    )

        def by_triple(d, h):
            return banks[d, h][:].rearrange("p t v -> p v t")

        on_vector_engine = nc.vector.tensor_copy
        on_scalar_engine = nc.scalar.copy

        for g in range(PASSES):
            quantise_w(0, g, 0, PACK, round_w(on_scalar_engine, 0, g, 0, PACK))
            product(0, g)

        low = round_w(on_vector_engine, 1, 0, 0, 2)
        high = round_w(on_scalar_engine, 1, 0, 2, PACK)
        quantise_w(1, 0, 2, PACK, high)
        quantise_w(1, 0, 0, 2, low)
        product(1, 0, (0,))
        rounded = keep.tile([P, PACK, P, PACK], BF16, name="w_bf1_1", align_bytes=64)
        dst = rounded[:].rearrange("p t (u q) j -> p t u j q", q=RUN)
        src = w_raw[1, 1].rearrange("p j (u t q) -> p t u j q", t=PACK, q=RUN)
        split = (H - SCALAR_COLS) // (PACK * RUN)
        nc.scalar.copy(out=dst[:, :, split:], in_=src[:, :, split:])
        for t0 in (0, 2):
            nc.vector.tensor_copy(out=dst[:, t0 : t0 + 2, :split], in_=src[:, t0 : t0 + 2, :split])
        for t0 in (0, 2):
            quantise_w(1, 1, t0, t0 + 2, rounded[:, t0 : t0 + 2])

        first = shared[:, first_start:].rearrange("p (v h t) -> p h v t", h=2, t=PACK)
        for h in range(2):
            nc.scalar.copy(out=first[:, h], in_=by_triple(0, h))
        product(1, 1, (0,))
        banks[1, 1] = psum.tile([P, PACK, HALF], F32, name="bank1_1", tag="bank0_1")
        for g in range(PASSES):
            product(1, g, (1,))

        low = [round_w(on_vector_engine, 2, 0, t, t + 1) for t in range(2)]
        high = round_w(on_scalar_engine, 2, 0, 2, PACK)
        for t in range(2):
            quantise_w(2, 0, t, t + 1, low[t])
        pair_first = keep.tile([P, HALF, PACK], F32, name="pair0", tag="w_bf2_0_0", align_bytes=64)
        nc.vector.tensor_tensor(pair_first[:], by_triple(1, 0), first[:, 0], MULT)
        quantise_w(2, 0, 2, PACK, high)
        product(2, 0)

        src = w_raw[LAST].rearrange("p j (u t q) -> p t u j q", t=PACK, q=RUN)
        low = keep.tile([P, 2, P, PACK], BF16, name="w_bf2_1_0", align_bytes=64)
        third = keep.tile([P, 1, P, PACK], BF16, name="w_bf2_1_2", tag="w_bf2_1_2", align_bytes=64)
        fourth = keep.tile([P, 1, P, PACK], BF16, name="w_bf2_1_3", align_bytes=64)
        rounded = (low[:, 0:1], low[:, 1:2], third[:], fourth[:])

        def round_last(copy, tile, t0, t1, c0, c1):
            groups = slice(c0 // (PACK * RUN), c1 // (PACK * RUN))
            copy(out=tile.rearrange("p t (u q) j -> p t u j q", q=RUN)[:, :, groups], in_=src[:, t0:t1, groups])

        round_last(on_vector_engine, low[:], 0, 2, 0, EARLY_COLS)
        round_last(on_vector_engine, rounded[2], 2, 3, 0, THIRD_SLOT_EARLY)
        round_last(on_scalar_engine, rounded[3], 3, 4, 0, EARLY_COLS)
        round_last(on_scalar_engine, rounded[2], 2, 3, THIRD_SLOT_EARLY, EARLY_COLS)
        round_last(on_vector_engine, rounded[0], 0, 1, EARLY_COLS, H)
        round_last(on_vector_engine, rounded[1], 1, 2, EARLY_COLS, H)
        round_last(on_vector_engine, rounded[2], 2, 3, EARLY_COLS, THIRD_SLOT_COLS)
        round_last(on_scalar_engine, rounded[2], 2, 3, THIRD_SLOT_COLS, H)
        round_last(on_scalar_engine, rounded[3], 3, 4, EARLY_COLS, H)
        for t in range(PACK):
            quantise_w(2, 1, t, t + 1, rounded[t])
        pair_second = keep.tile([P, HALF, PACK], F32, name="pair1", tag="w_raw2_1", align_bytes=DMA_ALIGN)
        nc.vector.tensor_tensor(pair_second[:], by_triple(1, 1), first[:, 1], MULT)
        product(2, 1)

        joint = keep.tile([P, N + HALF, PACK], BF16, name="joint", align_bytes=64)
        nc.scalar.copy(
            out=joint[:, :N].rearrange("p (c r) t -> p c t r", r=RUN),
            in_=w4_raw[:].rearrange("p t (c r) -> p c t r", r=RUN),
        )
        z_second = keep.tile([P, HALF, PACK], BF16, name="z_second", align_bytes=64)
        nc.vector.tensor_tensor(joint[:, N:], by_triple(2, 0), pair_first[:], MULT)
        own = HALF - GPSIMD_TRIPLES
        third_copy = keep.tile([P, GPSIMD_TRIPLES, PACK], F32, name="third_copy", tag="third_copy", align_bytes=64)
        nc.scalar.copy(out=third_copy[:], in_=by_triple(2, 1)[:, own:])
        nc.gpsimd.tensor_tensor(z_second[:, own:], third_copy[:], pair_second[:, own:], MULT)
        nc.vector.tensor_tensor(z_second[:, :own], by_triple(2, 1)[:, :own], pair_second[:, :own], MULT)
        w4_words = keep.tile([P, N], U32, name="w4_words", tag="third_copy", align_bytes=64)
        w4_scales = keep.tile([P, N], U8, name="w4_scales", align_bytes=64)
        first_words = keep.tile([P, HALF], U32, name="first_words", align_bytes=64)
        first_scales = keep.tile([P, HALF], U8, name="first_scales", align_bytes=64)
        for words, scales, cols in ((w4_words, w4_scales, slice(0, N)), (first_words, first_scales, slice(N, N + HALF))):
            nc.vector.quantize_mx(
                out=words[:].bitcast(FP8X4), scales=scales[:], in_=joint[:, cols].rearrange("p n t -> p (n t)")
            )
        second_words = keep.tile([P, HALF], U32, name="second_words", tag="w4_raw", align_bytes=DMA_ALIGN)
        second_scales = keep.tile([P, HALF], U8, name="second_scales", align_bytes=64)
        nc.vector.quantize_mx(
            out=second_words[:].bitcast(FP8X4), scales=second_scales[:], in_=z_second[:].rearrange("p v t -> p (v t)")
        )
        z_words = (first_words[:], second_words[:])
        z_scales = (first_scales[:], second_scales[:])
        results = [keep.tile([P, HALF], F32, name="result%d" % h, align_bytes=DMA_ALIGN) for h in range(2)]
        pieces = (
            (0, 0, HALF // 2, "acc0", on_vector_engine),
            (0, HALF // 2, HALF, "acc1", on_scalar_engine),
            (1, 0, HALF // 2, "bank0_0", on_vector_engine),
            (1, HALF // 2, HALF, "bank1_0", on_scalar_engine),
        )
        for h, c0, c1, bank, copy in pieces:
            acc = psum.tile([P, c1 - c0], F32, name="acc%d_%d" % (h, c0), tag=bank)
            nc.tensor.matmul_mx(
                out=acc[:],
                lhsT=w4_words[:].bitcast(FP8X4),
                lhsT_scale=w4_scales[:],
                rhs=z_words[h][:, c0:c1].bitcast(FP8X4),
                rhs_scale=z_scales[h][:, c0:c1],
                start=True,
                stop=True,
            )
            copy(out=results[h][:, c0:c1], in_=acc[:])
        for h, queue in enumerate((nc.sync, nc.scalar)):
            queue.dma_start(out=out[:, h * HALF : (h + 1) * HALF], in_=results[h][:])
